import numpy as np
import ml_dtypes


def mxq(x, axis, fmt="e4m3"):
    dtype, down = {"e4m3": (ml_dtypes.float8_e4m3fn, 7), "e5m2": (ml_dtypes.float8_e5m2, 14)}[fmt]
    v = np.moveaxis(np.asarray(x, np.float32).astype(ml_dtypes.bfloat16).astype(np.float64), axis, -1)
    blocks = v.reshape(v.shape[:-1] + (-1, 32))
    amax = np.abs(blocks).max(-1, keepdims=True)
    byte = np.maximum(np.where(amax > 0, np.frexp(amax)[1] - 1 + 127, 0) - down, 1)
    scale = np.exp2(byte - 127.0)
    codes = (blocks / scale).astype(np.float32).astype(dtype).astype(np.float64)
    return np.moveaxis((codes * scale).reshape(v.shape), -1, axis)


WIDE = False


def mx_kscale(k):
    if not WIDE:
        return np.ones(k)
    levels = np.array([10, -10, 5, -5, 0])
    if k % 512:
        return np.exp2(np.random.permutation(np.resize(levels, k // 32))).repeat(32)
    a = np.empty((k // 512, 16))
    for p in range(k // 512):
        a[p, :8] = np.random.permutation(np.resize(levels, 8))
        for g in range(8):
            far = levels[np.abs(levels - a[p, g]) >= 10]
            a[p, g + 8] = far[np.random.randint(len(far))]
    return np.exp2(a.ravel()).repeat(32)


BF16 = ml_dtypes.bfloat16


def bf(x):
    return np.asarray(x, np.float32).astype(BF16)


def f64(x):
    return np.asarray(x).astype(np.float64)

E4M3FN = np.array([(-1.0 if i & 128 else 1.0) * ((1.0 + (i & 7) / 8.0) * 2.0 ** (((i >> 3) & 15) - 7) if i & 120 else (i & 7) * 2.0 ** -9) for i in range(256)])


def e4m3fn_bytes(y):
    return np.clip(np.asarray(y, np.float64), -448.0, 448.0).astype(np.float32).astype(ml_dtypes.float8_e4m3fn).view(np.uint8)


def e4m3fn_values(b):
    return E4M3FN[b]

def planes(Y):
    n, m = Y.shape
    b = f64(bf(Y)).reshape(n // 32, 32, m)
    amax = np.abs(b).max(1)
    byte = np.clip(np.where(amax > 0, np.frexp(amax)[1] - 1 + 127 - 7, 1), 1, 254)
    codes = (b * np.exp2(127.0 - byte)[:, None, :]).reshape(n, m).astype(np.float32).astype(ml_dtypes.float8_e4m3fn).view(np.uint8)
    words = codes.reshape(n // 512, 128, 4, m).transpose(0, 1, 3, 2)
    return np.ascontiguousarray(words), np.ascontiguousarray(byte.astype(np.uint8).reshape(n // 512, 16, m))


T, K, F, B = 768, 1024, 4096, 128

E4M3_MAX = 448.0


def setup_inputs():
    s = mx_kscale(K)
    X = np.random.randn(T, K) * s
    X_scale = (np.abs(X).reshape(T, K // B, B).max(axis=2) / E4M3_MAX).astype(np.float32)
    X_bytes = e4m3fn_bytes(X / np.repeat(f64(X_scale), B, axis=1))
    c = 0.7 * np.exp(0.4 * np.random.randn(1, F))
    W = np.random.randn(K, F) / np.sqrt(K) / s[:, None] * c
    b = (1.0 + 0.3 * np.random.randn(1, F)) * c
    return {"X_bytes": X_bytes, "X_scale": X_scale, "W": bf(W), "b": bf(b)}


def reference(X_bytes, X_scale, W, b):
    X = e4m3fn_values(X_bytes) * np.repeat(f64(X_scale), B, axis=1)
    h = mxq(X, 1) @ mxq(f64(W), 0)
    a = np.maximum(h + f64(b), 0.0)
    y = np.square(a)
    words, scales = planes(y.T)
    return y, words, scales

@@ -1,0 +1,251 @@
+from contextlib import ExitStack
+
+import concourse.mybir as mybir
+from concourse.masks import make_identity
+
+T, K, F = 768, 1024, 4096
+FLOPS = 2 * T * K * F
+
+F32 = mybir.dt.float32
+BF16 = mybir.dt.bfloat16
+I32 = mybir.dt.int32
+U32 = mybir.dt.uint32
+U8 = mybir.dt.uint8
+FP8 = mybir.dt.float8_e4m3fn
+FP8X4 = mybir.dt.float8_e4m3fn_x4
+ACT = mybir.ActivationFunctionType
+ALU = mybir.AluOpType
+
+P = 128
+PACK = 4
+GROUP = P * PACK
+PASSES = K // GROUP
+GROUPS = F // GROUP
+HALF = T // 2
+TILES = HALF // P
+RUNS = (slice(0, 256), slice(256, HALF))
+STEPS = GROUPS * 2
+XBLOCK = 128
+XBLOCKS = K // XBLOCK
+EARLY_GROUPS = GROUPS - 2
+W_AHEAD = 3
+W_BUFS = 2
+HEAD_SPLIT = [32,32]
+GPSIMD_COLUMNS = 0
+SCALAR_RELU = [4]+[1,1,0]*4+[0]*3
+VECTOR_SQUARE = [0]*13+[128,128,256]
+
+
+def tile_squared_relu_up_projection_b1_kernel(tc, X_bytes, X_scale, W, b, out_0, out_1, out_2):
+    nc = tc.nc
+    with ExitStack() as ctx:
+        keep = ctx.enter_context(tc.tile_pool(name="keep", bufs=1))
+        work = ctx.enter_context(tc.tile_pool(name="work", bufs=3))
+        psum = ctx.enter_context(tc.psum_pool(name="psum", bufs=4))
+        ctx.enter_context(tc.manual_schedule())
+
+        ident = keep.tile([P, P], F32, name="ident")
+        make_identity(nc, ident[:])
+
+        x_scale = keep.tile([P, T // P, XBLOCKS], F32, name="x_scale")
+        bias = keep.tile([P, GROUPS, PACK], BF16, name="bias")
+        x_raw = [keep.tile([P, TILES, K], U8, name="x_raw%d" % h) for h in range(2)]
+        w_raw = [keep.tile([P, PACK, GROUP], BF16, name="w_raw%d" % n) for n in range(GROUPS * PASSES)]
+        x_grouped = [keep.tile([P, PASSES, HALF, PACK], BF16, name="x_grouped%d" % h, align_bytes=64) for h in range(2)]
+        x_codes = [keep.tile([P, PASSES, HALF], U32, name="x_codes%d" % h, align_bytes=64) for h in range(2)]
+        x_scales = [keep.tile([P, PASSES, HALF], U8, name="x_scales%d" % h, align_bytes=64) for h in range(2)]
+        y_scales_early = keep.tile([P, EARLY_GROUPS, T], U8, name="y_scales_early", align_bytes=64)
+        y_scales_last = keep.tile([P, GROUPS - EARLY_GROUPS, T], U8, name="y_scales_last", align_bytes=64)
+
+        def load_x(h):
+            nc.sync.dma_start(out=x_raw[h][:], in_=X_bytes[h * HALF:(h + 1) * HALF, :].rearrange("(i p) k -> p i k", p=P))
+
+        def load_w(n):
+            g, c = divmod(n, PASSES)
+            rows = W[c * GROUP:(c + 1) * GROUP, g * GROUP:(g + 1) * GROUP]
+            nc.sync.dma_start(out=w_raw[n][:], in_=rows.rearrange("(p j) n -> p j n", j=PACK))
+
+        nc.sync.dma_start(out=x_scale[:], in_=X_scale.rearrange("(i p) j -> p i j", p=P))
+        load_x(0)
+        load_w(0)
+        load_w(1)
+        load_x(1)
+        nc.sync.dma_start(out=bias[:], in_=b.rearrange("o (g p t) -> p (o g) t", p=P, t=PACK))
+        for n in range(PASSES, GROUPS * PASSES):
+            load_w(n)
+
+        x_wide, w_grouped, w_codes, w_scales = {}, {}, {}, {}
+        h_banks, act, turned, y_bf16 = {}, {}, {}, {}
+
+        def widen_x(h, i, on_vector):
+            for c in range(PASSES):
+                wide = work.tile([P, GROUP], BF16, name="x_wide", bufs=PASSES * 2 * TILES)
+                x_wide[h, i, c] = (wide, on_vector)
+                for q in range(GROUP // XBLOCK):
+                    j = c * (GROUP // XBLOCK) + q
+                    src = x_raw[h][:, i, j * XBLOCK:(j + 1) * XBLOCK].bitcast(FP8)
+                    dst = wide[:, q * XBLOCK:(q + 1) * XBLOCK]
+                    scale = x_scale[:, h * TILES + i, j:j + 1]
+                    if on_vector:
+                        dst = wide[:].rearrange("p (u q a e) -> p q a u e", u=2, q=4, e=2)[:, q]
+                        nc.vector.tensor_scalar(out=dst, in0=src.rearrange("p (a u e) -> p a u e", u=2, e=2),
+                                                scalar1=scale, scalar2=None, op0=ALU.mult)
+                    else:
+                        nc.scalar.activation(out=dst, in_=src, func=ACT.Copy, scale=scale)
+
+        def turn_x(h, i):
+            pairs = x_grouped[h][:].rearrange("p c m t -> p c (m t)").bitcast(F32).rearrange("p c (m u) -> p c m u", u=2)
+            bank = psum.tile([P, GROUP], F32, name="turn")
+            for c in range(PASSES):
+                wide, is_sorted = x_wide[h, i, c]
+                words = wide[:].bitcast(F32)
+                for u in range(2):
+                    col = (2 * c + u) * P
+                    src = words[:, u * P:(u + 1) * P] if is_sorted else words[:, u:GROUP // 2:2]
+                    nc.tensor.transpose(bank[:, col:col + P], src, ident[:])
+            nc.scalar.copy(out=pairs[:, :, i * P:(i + 1) * P, :],
+                           in_=bank[:].rearrange("p (c u m) -> p c m u", c=PASSES, u=2))
+
+        def quantize_x(h):
+            for c in range(PASSES):
+                for run in RUNS:
+                    nc.vector.quantize_mx(out=x_codes[h][:, c, run].bitcast(FP8X4), scales=x_scales[h][:, c, run],
+                                          in_=x_grouped[h][:, c, run, :].rearrange("p m t -> p (m t)"))
+
+        def interleave_w(n, split, helper):
+            head = n < W_AHEAD
+            grouped = work.tile([P, PACK, P, PACK], BF16, name="w_head" if head else "w_grouped", bufs=2 if head else W_BUFS, align_bytes=64)
+            w_grouped[n] = grouped
+            if split and helper == "scalar":
+                nc.scalar.copy(out=grouped[:, :, :split, :].rearrange("p t (a i) j -> p a t i j", i=2),
+                               in_=w_raw[n][:, :, :PACK * split].rearrange("p j (a i t) -> p a t i j", i=2, t=PACK))
+            elif split:
+                nc.gpsimd.tensor_scalar(out=grouped[:, :, :split, :].rearrange("p t m j -> p m t j"),
+                                        in0=w_raw[n][:, :, :PACK * split].rearrange("p j (m t) -> p m t j", t=PACK),
+                                        scalar1=1.0, scalar2=0.0, op0=ALU.mult, op1=ALU.add)
+            nc.vector.tensor_copy(
+                out=grouped[:, :, split:, :].rearrange("p t (a i) j -> p a t i j", i=2),
+                in_=w_raw[n][:, :, PACK * split:].rearrange("p j (a i t) -> p a t i j", i=2, t=PACK))
+
+        def quantize_w(n):
+            w_codes[n] = work.tile([P, GROUP], U32, name="w_codes", bufs=6, align_bytes=64)
+            w_scales[n] = work.tile([P, GROUP], U8, name="w_scales", bufs=6, align_bytes=64)
+            nc.vector.quantize_mx(out=w_codes[n][:].bitcast(FP8X4), scales=w_scales[n][:],
+                                  in_=w_grouped[n][:].rearrange("p t m j -> p (t m j)"))
+
+        def multiply(step, t):
+            g, h = divmod(step, 2)
+            bank = psum.tile([P, GROUP], F32, name="h")
+            h_banks[step, t] = bank
+            cols = slice(t * P, (t + 1) * P)
+            for run in RUNS:
+                for c in range(PASSES):
+                    n = g * PASSES + c
+                    nc.tensor.matmul_mx(out=bank[:, run],
+                                        lhsT=w_codes[n][:, cols].bitcast(FP8X4), lhsT_scale=w_scales[n][:, cols],
+                                        rhs=x_codes[h][:, c, run].bitcast(FP8X4), rhs_scale=x_scales[h][:, c, run],
+                                        start=(c == 0), stop=(c == PASSES - 1))
+
+        def rectify(step, t, on_vector):
+            g = step // 2
+            if t == 0:
+                act[step] = work.tile([P, PACK, HALF], F32, name="act")
+            src = h_banks[step, t][:, :HALF]
+            if on_vector:
+                nc.vector.tensor_scalar(out=act[step][:, t, :], in0=src, scalar1=bias[:, g, t:t + 1], scalar2=0.0,
+                                        op0=ALU.add, op1=ALU.max)
+            else:
+                nc.scalar.activation(out=act[step][:, t, :], in_=src, func=ACT.Relu, bias=bias[:, g, t:t + 1])
+
+        def turn_act(step, i):
+            bank = psum.tile([P, GROUP], F32, name="turn")
+            turned[step, i] = bank
+            for t in range(PACK):
+                nc.tensor.transpose(bank[:, t * P:(t + 1) * P], act[step][:, t, i * P:(i + 1) * P], ident[:])
+
+        def square_for_planes(step):
+            y_bf16[step] = work.tile([P, HALF, PACK], BF16, name="y_bf16", align_bytes=64)
+            dst = y_bf16[step][:].rearrange("p (a i) t -> p a t i", i=4)
+            src = act[step][:].rearrange("p t (a i) -> p a t i", i=4)
+            cut = (HALF - VECTOR_SQUARE[step]) // 4
+            if cut > 0:
+                nc.scalar.activation(out=dst[:, :cut], in_=src[:, :cut], func=ACT.Square)
+            if cut < HALF // 4:
+                nc.vector.tensor_tensor(out=dst[:, cut:], in0=src[:, cut:], in1=src[:, cut:], op=ALU.mult)
+
+        def square_and_store(step):
+            g, h = divmod(step, 2)
+            y = work.tile([P, TILES, GROUP], F32, name="y", bufs=6)
+            dst = out_0[h * HALF:(h + 1) * HALF, g * GROUP:(g + 1) * GROUP].rearrange("(i p) f -> p i f", p=P)
+            for i in range(TILES):
+                nc.scalar.activation(out=y[:, i, :].rearrange("p (m t) -> p m t", t=PACK),
+                                     in_=turned[step, i][:].rearrange("p (t m) -> p m t", t=PACK), func=ACT.Square)
+                if step >= STEPS - 2:
+                    if step == STEPS - 1 and i == 2:
+                        quantize_y(step)
+                    queue = nc.scalar if step == STEPS - 1 and i == TILES - 1 else nc.sync
+                    queue.dma_start(out=dst[:, i, :], in_=y[:, i, :])
+            if step < STEPS - 2:
+                nc.sync.dma_start(out=dst, in_=y[:])
+
+        def store_scales(plane, g0, g1):
+            for quad in range(4):
+                dst = out_2[g0:g1, 4 * quad:4 * quad + 4, :].rearrange("g r m -> r g m")
+                nc.sync.dma_start(out=dst.bitcast(I32), in_=plane[32 * quad:32 * quad + 4, :, :].bitcast(I32))
+
+        def quantize_y(step):
+            g, h = divmod(step, 2)
+            tokens = slice(h * HALF, (h + 1) * HALF)
+            codes = work.tile([P, HALF], U32, name="y_codes", bufs=6, align_bytes=64)
+            plane = y_scales_last[:, g - EARLY_GROUPS, tokens] if g >= EARLY_GROUPS else y_scales_early[:, g, tokens]
+            for run in RUNS:
+                nc.vector.quantize_mx(out=codes[:, run].bitcast(FP8X4), scales=plane[:, run],
+                                      in_=y_bf16[step][:, run, :].rearrange("p m t -> p (m t)"))
+            dst = out_1[g, :, tokens, :].rearrange("p m t -> p (m t)")
+            nc.sync.dma_start(out=dst.bitcast(I32), in_=codes[:].bitcast(I32))
+            if step == 2 * EARLY_GROUPS - 1:
+                store_scales(y_scales_early, 0, EARLY_GROUPS)
+            if step == STEPS - 1:
+                store_scales(y_scales_last, EARLY_GROUPS, GROUPS)
+
+        widen_x(0, 0, True)
+        widen_x(0, 2, False)
+        widen_x(0, 1, True)
+        turn_x(0, 0)
+        interleave_w(0, HEAD_SPLIT[0], "scalar")
+        turn_x(0, 1)
+        turn_x(0, 2)
+        interleave_w(1, HEAD_SPLIT[1], "scalar")
+        quantize_w(0)
+        quantize_x(0)
+        quantize_w(1)
+        for t in range(PACK):
+            multiply(0, t)
+        for i in range(TILES):
+            widen_x(1, i, True)
+        interleave_w(2, 0, None)
+
+        for step in range(STEPS):
+            for t in range(PACK):
+                rectify(step, t, t < PACK - SCALAR_RELU[step])
+            n = step + W_AHEAD
+            if step == 0:
+                for i in range(TILES):
+                    turn_x(1, i)
+                quantize_w(2)
+            if n < GROUPS * PASSES:
+                interleave_w(n, GPSIMD_COLUMNS if step else 0, "gpsimd")
+            if step > 0:
+                quantize_y(step - 1)
+            else:
+                quantize_x(1)
+            if n < GROUPS * PASSES:
+                quantize_w(n)
+            for t in range(PACK):
+                if t == (2 if step else 0):
+                    for i in range(TILES):
+                        turn_act(step, i)
+                if step + 1 < STEPS:
+                    multiply(step + 1, t)
+            square_for_planes(step)
+            square_and_store(step)

@@ -29,10 +29,10 @@ XBLOCK = 128
 XBLOCKS = K // XBLOCK
 EARLY_GROUPS = GROUPS - 2
 W_AHEAD = 3
-W_BUFS = 2
+W_BUFS = 1
 HEAD_SPLIT = [32,32]
-GPSIMD_COLUMNS = 0
-SCALAR_RELU = [4]+[1,1,0]*4+[0]*3
+GPSIMD_COLUMNS = 56
+SCALAR_RELU = [4]+[0]*15
 VECTOR_SQUARE = [0]*13+[128,128,256]
 
 
@@ -47,7 +47,7 @@ def tile_squared_relu_up_projection_b1_kernel(tc, X_bytes, X_scale, W, b, out_0,
         ident = keep.tile([P, P], F32, name="ident")
         make_identity(nc, ident[:])
 
-        x_scale = keep.tile([P, T // P, XBLOCKS], F32, name="x_scale")
+        x_scale = [keep.tile([P, TILES, XBLOCKS], F32, name="x_scale%d" % h) for h in range(2)]
         bias = keep.tile([P, GROUPS, PACK], BF16, name="bias")
         x_raw = [keep.tile([P, TILES, K], U8, name="x_raw%d" % h) for h in range(2)]
         w_raw = [keep.tile([P, PACK, GROUP], BF16, name="w_raw%d" % n) for n in range(GROUPS * PASSES)]
@@ -58,6 +58,7 @@ def tile_squared_relu_up_projection_b1_kernel(tc, X_bytes, X_scale, W, b, out_0,
         y_scales_last = keep.tile([P, GROUPS - EARLY_GROUPS, T], U8, name="y_scales_last", align_bytes=64)
 
         def load_x(h):
+            nc.sync.dma_start(out=x_scale[h][:], in_=X_scale[h * HALF:(h + 1) * HALF, :].rearrange("(i p) j -> p i j", p=P))
             nc.sync.dma_start(out=x_raw[h][:], in_=X_bytes[h * HALF:(h + 1) * HALF, :].rearrange("(i p) k -> p i k", p=P))
 
         def load_w(n):
@@ -65,7 +66,6 @@ def tile_squared_relu_up_projection_b1_kernel(tc, X_bytes, X_scale, W, b, out_0,
             rows = W[c * GROUP:(c + 1) * GROUP, g * GROUP:(g + 1) * GROUP]
             nc.sync.dma_start(out=w_raw[n][:], in_=rows.rearrange("(p j) n -> p j n", j=PACK))
 
-        nc.sync.dma_start(out=x_scale[:], in_=X_scale.rearrange("(i p) j -> p i j", p=P))
         load_x(0)
         load_w(0)
         load_w(1)
@@ -85,7 +85,7 @@ def tile_squared_relu_up_projection_b1_kernel(tc, X_bytes, X_scale, W, b, out_0,
                     j = c * (GROUP // XBLOCK) + q
                     src = x_raw[h][:, i, j * XBLOCK:(j + 1) * XBLOCK].bitcast(FP8)
                     dst = wide[:, q * XBLOCK:(q + 1) * XBLOCK]
-                    scale = x_scale[:, h * TILES + i, j:j + 1]
+                    scale = x_scale[h][:, i, j:j + 1]
                     if on_vector:
                         dst = wide[:].rearrange("p (u q a e) -> p q a u e", u=2, q=4, e=2)[:, q]
                         nc.vector.tensor_scalar(out=dst, in0=src.rearrange("p (a u e) -> p a u e", u=2, e=2),
@@ -222,7 +222,7 @@ def tile_squared_relu_up_projection_b1_kernel(tc, X_bytes, X_scale, W, b, out_0,
         for t in range(PACK):
             multiply(0, t)
         for i in range(TILES):
-            widen_x(1, i, True)
+            widen_x(1, i, i >= 2)
         interleave_w(2, 0, None)
 
         for step in range(STEPS):
@@ -241,11 +241,18 @@ def tile_squared_relu_up_projection_b1_kernel(tc, X_bytes, X_scale, W, b, out_0,
                 quantize_x(1)
             if n < GROUPS * PASSES:
                 quantize_w(n)
-            for t in range(PACK):
-                if t == (2 if step else 0):
-                    for i in range(TILES):
-                        turn_act(step, i)
-                if step + 1 < STEPS:
+            if 0 < step < STEPS - 1:
+                for t in range(PACK - 1):
                     multiply(step + 1, t)
+                turn_act(step, 0)
+                turn_act(step, 1)
+                multiply(step + 1, PACK - 1)
+                turn_act(step, 2)
+            else:
+                for i in range(TILES):
+                    turn_act(step, i)
+                if step == 0:
+                    for t in range(PACK):
+                        multiply(1, t)
             square_for_planes(step)
             square_and_store(step)

@@ -31,9 +31,9 @@ EARLY_GROUPS = GROUPS - 2
 W_AHEAD = 3
 W_BUFS = 1
 HEAD_SPLIT = [32,32]
-GPSIMD_COLUMNS = 56
-SCALAR_RELU = [4]+[0]*15
-VECTOR_SQUARE = [0]*13+[128,128,256]
+GPSIMD_COLUMNS = [64]*13
+SCALAR_RELU = [0]*16
+VECTOR_SQUARE = [0]*13+[96,96,256]
 
 
 def tile_squared_relu_up_projection_b1_kernel(tc, X_bytes, X_scale, W, b, out_0, out_1, out_2):
@@ -49,7 +49,8 @@ def tile_squared_relu_up_projection_b1_kernel(tc, X_bytes, X_scale, W, b, out_0,
 
         x_scale = [keep.tile([P, TILES, XBLOCKS], F32, name="x_scale%d" % h) for h in range(2)]
         bias = keep.tile([P, GROUPS, PACK], BF16, name="bias")
-        x_raw = [keep.tile([P, TILES, K], U8, name="x_raw%d" % h) for h in range(2)]
+        x_raw = [keep.tile([P, K], U8, name="x_raw%d" % i) for i in range(TILES)]
+        x_raw_late = keep.tile([P, TILES, K], U8, name="x_raw_late")
         w_raw = [keep.tile([P, PACK, GROUP], BF16, name="w_raw%d" % n) for n in range(GROUPS * PASSES)]
         x_grouped = [keep.tile([P, PASSES, HALF, PACK], BF16, name="x_grouped%d" % h, align_bytes=64) for h in range(2)]
         x_codes = [keep.tile([P, PASSES, HALF], U32, name="x_codes%d" % h, align_bytes=64) for h in range(2)]
@@ -57,19 +58,21 @@ def tile_squared_relu_up_projection_b1_kernel(tc, X_bytes, X_scale, W, b, out_0,
         y_scales_early = keep.tile([P, EARLY_GROUPS, T], U8, name="y_scales_early", align_bytes=64)
         y_scales_last = keep.tile([P, GROUPS - EARLY_GROUPS, T], U8, name="y_scales_last", align_bytes=64)
 
-        def load_x(h):
-            nc.sync.dma_start(out=x_scale[h][:], in_=X_scale[h * HALF:(h + 1) * HALF, :].rearrange("(i p) j -> p i j", p=P))
-            nc.sync.dma_start(out=x_raw[h][:], in_=X_bytes[h * HALF:(h + 1) * HALF, :].rearrange("(i p) k -> p i k", p=P))
+        def load_x_scale(h, queue):
+            queue.dma_start(out=x_scale[h][:], in_=X_scale[h * HALF:(h + 1) * HALF, :].rearrange("(i p) j -> p i j", p=P))
 
         def load_w(n):
             g, c = divmod(n, PASSES)
             rows = W[c * GROUP:(c + 1) * GROUP, g * GROUP:(g + 1) * GROUP]
             nc.sync.dma_start(out=w_raw[n][:], in_=rows.rearrange("(p j) n -> p j n", j=PACK))
 
-        load_x(0)
+        load_x_scale(0, nc.scalar)
+        for i in (0, 2, 1):
+            nc.sync.dma_start(out=x_raw[i][:], in_=X_bytes[i * P:(i + 1) * P, :])
         load_w(0)
         load_w(1)
-        load_x(1)
+        load_x_scale(1, nc.sync)
+        nc.sync.dma_start(out=x_raw_late[:], in_=X_bytes[HALF:, :].rearrange("(i p) k -> p i k", p=P))
         nc.sync.dma_start(out=bias[:], in_=b.rearrange("o (g p t) -> p (o g) t", p=P, t=PACK))
         for n in range(PASSES, GROUPS * PASSES):
             load_w(n)
@@ -83,7 +86,8 @@ def tile_squared_relu_up_projection_b1_kernel(tc, X_bytes, X_scale, W, b, out_0,
                 x_wide[h, i, c] = (wide, on_vector)
                 for q in range(GROUP // XBLOCK):
                     j = c * (GROUP // XBLOCK) + q
-                    src = x_raw[h][:, i, j * XBLOCK:(j + 1) * XBLOCK].bitcast(FP8)
+                    row = x_raw_late[:, i, :] if h else x_raw[i][:]
+                    src = row[:, j * XBLOCK:(j + 1) * XBLOCK].bitcast(FP8)
                     dst = wide[:, q * XBLOCK:(q + 1) * XBLOCK]
                     scale = x_scale[h][:, i, j:j + 1]
                     if on_vector:
@@ -93,7 +97,7 @@ def tile_squared_relu_up_projection_b1_kernel(tc, X_bytes, X_scale, W, b, out_0,
                     else:
                         nc.scalar.activation(out=dst, in_=src, func=ACT.Copy, scale=scale)
 
-        def turn_x(h, i):
+        def turn_x(h, i, on_vector=False):
             pairs = x_grouped[h][:].rearrange("p c m t -> p c (m t)").bitcast(F32).rearrange("p c (m u) -> p c m u", u=2)
             bank = psum.tile([P, GROUP], F32, name="turn")
             for c in range(PASSES):
@@ -103,17 +107,17 @@ def tile_squared_relu_up_projection_b1_kernel(tc, X_bytes, X_scale, W, b, out_0,
                     col = (2 * c + u) * P
                     src = words[:, u * P:(u + 1) * P] if is_sorted else words[:, u:GROUP // 2:2]
                     nc.tensor.transpose(bank[:, col:col + P], src, ident[:])
-            nc.scalar.copy(out=pairs[:, :, i * P:(i + 1) * P, :],
-                           in_=bank[:].rearrange("p (c u m) -> p c m u", c=PASSES, u=2))
+            copy = nc.vector.tensor_copy if on_vector else nc.scalar.copy
+            copy(out=pairs[:, :, i * P:(i + 1) * P, :], in_=bank[:].rearrange("p (c u m) -> p c m u", c=PASSES, u=2))
 
         def quantize_x(h):
-            for c in range(PASSES):
-                for run in RUNS:
-                    nc.vector.quantize_mx(out=x_codes[h][:, c, run].bitcast(FP8X4), scales=x_scales[h][:, c, run],
-                                          in_=x_grouped[h][:, c, run, :].rearrange("p m t -> p (m t)"))
+            for run in (slice(0, 512), slice(512, PASSES * HALF)):
+                nc.vector.quantize_mx(out=x_codes[h][:].rearrange("p c m -> p (c m)")[:, run].bitcast(FP8X4),
+                                      scales=x_scales[h][:].rearrange("p c m -> p (c m)")[:, run],
+                                      in_=x_grouped[h][:].rearrange("p c m t -> p (c m) t")[:, run, :].rearrange("p m t -> p (m t)"))
 
         def interleave_w(n, split, helper):
-            head = n < W_AHEAD
+            head = n < PASSES
             grouped = work.tile([P, PACK, P, PACK], BF16, name="w_head" if head else "w_grouped", bufs=2 if head else W_BUFS, align_bytes=64)
             w_grouped[n] = grouped
             if split and helper == "scalar":
@@ -124,8 +128,8 @@ def tile_squared_relu_up_projection_b1_kernel(tc, X_bytes, X_scale, W, b, out_0,
                                         in0=w_raw[n][:, :, :PACK * split].rearrange("p j (m t) -> p m t j", t=PACK),
                                         scalar1=1.0, scalar2=0.0, op0=ALU.mult, op1=ALU.add)
             nc.vector.tensor_copy(
-                out=grouped[:, :, split:, :].rearrange("p t (a i) j -> p a t i j", i=2),
-                in_=w_raw[n][:, :, PACK * split:].rearrange("p j (a i t) -> p a t i j", i=2, t=PACK))
+                out=grouped[:, :, split:, :].rearrange("p t m j -> p m j t"),
+                in_=w_raw[n][:, :, PACK * split:].rearrange("p j (m t) -> p m j t", t=PACK))
 
         def quantize_w(n):
             w_codes[n] = work.tile([P, GROUP], U32, name="w_codes", bufs=6, align_bytes=64)
@@ -164,8 +168,10 @@ def tile_squared_relu_up_projection_b1_kernel(tc, X_bytes, X_scale, W, b, out_0,
                 nc.tensor.transpose(bank[:, t * P:(t + 1) * P], act[step][:, t, i * P:(i + 1) * P], ident[:])
 
         def square_for_planes(step):
-            y_bf16[step] = work.tile([P, HALF, PACK], BF16, name="y_bf16", align_bytes=64)
-            dst = y_bf16[step][:].rearrange("p (a i) t -> p a t i", i=4)
+            g, h = divmod(step, 2)
+            if h == 0:
+                y_bf16[g] = work.tile([P, T, PACK], BF16, name="y_bf16", bufs=2, align_bytes=64)
+            dst = y_bf16[g][:, h * HALF:(h + 1) * HALF, :].rearrange("p (a i) t -> p a t i", i=4)
             src = act[step][:].rearrange("p t (a i) -> p a t i", i=4)
             cut = (HALF - VECTOR_SQUARE[step]) // 4
             if cut > 0:
@@ -180,13 +186,7 @@ def tile_squared_relu_up_projection_b1_kernel(tc, X_bytes, X_scale, W, b, out_0,
             for i in range(TILES):
                 nc.scalar.activation(out=y[:, i, :].rearrange("p (m t) -> p m t", t=PACK),
                                      in_=turned[step, i][:].rearrange("p (t m) -> p m t", t=PACK), func=ACT.Square)
-                if step >= STEPS - 2:
-                    if step == STEPS - 1 and i == 2:
-                        quantize_y(step)
-                    queue = nc.scalar if step == STEPS - 1 and i == TILES - 1 else nc.sync
-                    queue.dma_start(out=dst[:, i, :], in_=y[:, i, :])
-            if step < STEPS - 2:
-                nc.sync.dma_start(out=dst, in_=y[:])
+                nc.sync.dma_start(out=dst[:, i, :], in_=y[:, i, :])
 
         def store_scales(plane, g0, g1):
             for quad in range(4):
@@ -195,13 +195,17 @@ def tile_squared_relu_up_projection_b1_kernel(tc, X_bytes, X_scale, W, b, out_0,
 
         def quantize_y(step):
             g, h = divmod(step, 2)
-            tokens = slice(h * HALF, (h + 1) * HALF)
-            codes = work.tile([P, HALF], U32, name="y_codes", bufs=6, align_bytes=64)
-            plane = y_scales_last[:, g - EARLY_GROUPS, tokens] if g >= EARLY_GROUPS else y_scales_early[:, g, tokens]
-            for run in RUNS:
-                nc.vector.quantize_mx(out=codes[:, run].bitcast(FP8X4), scales=plane[:, run],
-                                      in_=y_bf16[step][:, run, :].rearrange("p m t -> p (m t)"))
-            dst = out_1[g, :, tokens, :].rearrange("p m t -> p (m t)")
+            if g < GROUPS - 1:
+                runs = [(slice(0, 256), slice(256, T))[h]]
+            else:
+                runs = [slice(h * HALF + run.start, h * HALF + run.stop) for run in RUNS]
+            first, last = runs[0].start, runs[-1].stop
+            codes = work.tile([P, last - first], U32, name="y_codes", bufs=6, align_bytes=64)
+            plane = y_scales_last[:, g - EARLY_GROUPS, :] if g >= EARLY_GROUPS else y_scales_early[:, g, :]
+            for run in runs:
+                nc.vector.quantize_mx(out=codes[:, run.start - first:run.stop - first].bitcast(FP8X4), scales=plane[:, run],
+                                      in_=y_bf16[g][:, run, :].rearrange("p m t -> p (m t)"))
+            dst = out_1[g, :, first:last, :].rearrange("p m t -> p (m t)")
             nc.sync.dma_start(out=dst.bitcast(I32), in_=codes[:].bitcast(I32))
             if step == 2 * EARLY_GROUPS - 1:
                 store_scales(y_scales_early, 0, EARLY_GROUPS)
@@ -221,27 +225,28 @@ def tile_squared_relu_up_projection_b1_kernel(tc, X_bytes, X_scale, W, b, out_0,
         quantize_w(1)
         for t in range(PACK):
             multiply(0, t)
-        for i in range(TILES):
-            widen_x(1, i, i >= 2)
+        widen_x(1, 0, False)
+        widen_x(1, 1, False)
         interleave_w(2, 0, None)
+        widen_x(1, 2, True)
+        quantize_w(2)
+        turn_x(1, 0)
+        turn_x(1, 1)
+        turn_x(1, 2)
 
         for step in range(STEPS):
             for t in range(PACK):
                 rectify(step, t, t < PACK - SCALAR_RELU[step])
             n = step + W_AHEAD
             if step == 0:
-                for i in range(TILES):
-                    turn_x(1, i)
-                quantize_w(2)
-            if n < GROUPS * PASSES:
-                interleave_w(n, GPSIMD_COLUMNS if step else 0, "gpsimd")
-            if step > 0:
-                quantize_y(step - 1)
-            else:
                 quantize_x(1)
             if n < GROUPS * PASSES:
+                interleave_w(n, GPSIMD_COLUMNS[step], "gpsimd")
+            if step > 0:
+                quantize_y(step - 1)
+            if n < GROUPS * PASSES:
                 quantize_w(n)
-            if 0 < step < STEPS - 1:
+            if step < STEPS - 1:
                 for t in range(PACK - 1):
                     multiply(step + 1, t)
                 turn_act(step, 0)
@@ -251,8 +256,6 @@ def tile_squared_relu_up_projection_b1_kernel(tc, X_bytes, X_scale, W, b, out_0,
             else:
                 for i in range(TILES):
                     turn_act(step, i)
-                if step == 0:
-                    for t in range(PACK):
-                        multiply(1, t)
             square_for_planes(step)
             square_and_store(step)
+        quantize_y(STEPS - 1)

@@ -31,7 +31,7 @@ EARLY_GROUPS = GROUPS - 2
 W_AHEAD = 3
 W_BUFS = 1
 HEAD_SPLIT = [32,32]
-GPSIMD_COLUMNS = [64]*13
+GPSIMD_COLUMNS = [60]*13
 SCALAR_RELU = [0]*16
 VECTOR_SQUARE = [0]*13+[96,96,256]
 
@@ -171,12 +171,12 @@ def tile_squared_relu_up_projection_b1_kernel(tc, X_bytes, X_scale, W, b, out_0,
             g, h = divmod(step, 2)
             if h == 0:
                 y_bf16[g] = work.tile([P, T, PACK], BF16, name="y_bf16", bufs=2, align_bytes=64)
-            dst = y_bf16[g][:, h * HALF:(h + 1) * HALF, :].rearrange("p (a i) t -> p a t i", i=4)
-            src = act[step][:].rearrange("p t (a i) -> p a t i", i=4)
-            cut = (HALF - VECTOR_SQUARE[step]) // 4
+            dst = y_bf16[g][:, h * HALF:(h + 1) * HALF, :].rearrange("p (a i) t -> p a t i", i=2)
+            src = act[step][:].rearrange("p t (a i) -> p a t i", i=2)
+            cut = (HALF - VECTOR_SQUARE[step]) // 2
             if cut > 0:
                 nc.scalar.activation(out=dst[:, :cut], in_=src[:, :cut], func=ACT.Square)
-            if cut < HALF // 4:
+            if cut < HALF // 2:
                 nc.vector.tensor_tensor(out=dst[:, cut:], in0=src[:, cut:], in1=src[:, cut:], op=ALU.mult)
 
         def square_and_store(step):

@@ -21,19 +21,23 @@ PACK = 4
 GROUP = P * PACK
 PASSES = K // GROUP
 GROUPS = F // GROUP
+W_TILES = GROUPS * PASSES
 HALF = T // 2
 TILES = HALF // P
+STEPS = 2 * GROUPS
 RUNS = (slice(0, 256), slice(256, HALF))
-STEPS = GROUPS * 2
-XBLOCK = 128
-XBLOCKS = K // XBLOCK
-EARLY_GROUPS = GROUPS - 2
+X_BLOCK = 128
+QUADRANTS = 4
+
 W_AHEAD = 3
-W_BUFS = 1
-HEAD_SPLIT = [32,32]
-GPSIMD_COLUMNS = [60]*13
-SCALAR_RELU = [0]*16
-VECTOR_SQUARE = [0]*13+[96,96,256]
+GPSIMD_SHARE = 64
+SCALAR_SHARE = 4
+HEAD_SCALAR_SHARE = 32
+VECTOR_TOKENS_LATE = 96
+VECTOR_TOKENS_LAST = 256
+EARLY_GROUPS = GROUPS - 2
+W_CODE_SLOTS = 3 * PASSES
+RESULT_SLOTS = 6
 
 
 def tile_squared_relu_up_projection_b1_kernel(tc, X_bytes, X_scale, W, b, out_0, out_1, out_2):
@@ -47,19 +51,20 @@ def tile_squared_relu_up_projection_b1_kernel(tc, X_bytes, X_scale, W, b, out_0,
         ident = keep.tile([P, P], F32, name="ident")
         make_identity(nc, ident[:])
 
-        x_scale = [keep.tile([P, TILES, XBLOCKS], F32, name="x_scale%d" % h) for h in range(2)]
+        x_scale = [keep.tile([P, TILES, K // X_BLOCK], F32, name="x_scale%d" % h) for h in range(2)]
         bias = keep.tile([P, GROUPS, PACK], BF16, name="bias")
-        x_raw = [keep.tile([P, K], U8, name="x_raw%d" % i) for i in range(TILES)]
-        x_raw_late = keep.tile([P, TILES, K], U8, name="x_raw_late")
-        w_raw = [keep.tile([P, PACK, GROUP], BF16, name="w_raw%d" % n) for n in range(GROUPS * PASSES)]
+        x_raw_first = [keep.tile([P, K], U8, name="x_raw_first%d" % i) for i in range(TILES)]
+        x_raw_second = keep.tile([P, TILES, K], U8, name="x_raw_second")
+        w_raw = [keep.tile([P, PACK, GROUP], BF16, name="w_raw%d" % n) for n in range(W_TILES)]
         x_grouped = [keep.tile([P, PASSES, HALF, PACK], BF16, name="x_grouped%d" % h, align_bytes=64) for h in range(2)]
         x_codes = [keep.tile([P, PASSES, HALF], U32, name="x_codes%d" % h, align_bytes=64) for h in range(2)]
         x_scales = [keep.tile([P, PASSES, HALF], U8, name="x_scales%d" % h, align_bytes=64) for h in range(2)]
         y_scales_early = keep.tile([P, EARLY_GROUPS, T], U8, name="y_scales_early", align_bytes=64)
-        y_scales_last = keep.tile([P, GROUPS - EARLY_GROUPS, T], U8, name="y_scales_last", align_bytes=64)
+        y_scales_late = keep.tile([P, GROUPS - EARLY_GROUPS, T], U8, name="y_scales_late", align_bytes=64)
 
         def load_x_scale(h, queue):
-            queue.dma_start(out=x_scale[h][:], in_=X_scale[h * HALF:(h + 1) * HALF, :].rearrange("(i p) j -> p i j", p=P))
+            rows = X_scale[h * HALF:(h + 1) * HALF, :]
+            queue.dma_start(out=x_scale[h][:], in_=rows.rearrange("(i p) j -> p i j", p=P))
 
         def load_w(n):
             g, c = divmod(n, PASSES)
@@ -68,72 +73,75 @@ def tile_squared_relu_up_projection_b1_kernel(tc, X_bytes, X_scale, W, b, out_0,
 
         load_x_scale(0, nc.scalar)
         for i in (0, 2, 1):
-            nc.sync.dma_start(out=x_raw[i][:], in_=X_bytes[i * P:(i + 1) * P, :])
+            nc.sync.dma_start(out=x_raw_first[i][:], in_=X_bytes[i * P:(i + 1) * P, :])
         load_w(0)
-        load_w(1)
         load_x_scale(1, nc.sync)
-        nc.sync.dma_start(out=x_raw_late[:], in_=X_bytes[HALF:, :].rearrange("(i p) k -> p i k", p=P))
+        nc.sync.dma_start(out=x_raw_second[:], in_=X_bytes[HALF:, :].rearrange("(i p) k -> p i k", p=P))
+        load_w(1)
         nc.sync.dma_start(out=bias[:], in_=b.rearrange("o (g p t) -> p (o g) t", p=P, t=PACK))
-        for n in range(PASSES, GROUPS * PASSES):
+        for n in range(PASSES, W_TILES):
             load_w(n)
 
-        x_wide, w_grouped, w_codes, w_scales = {}, {}, {}, {}
-        h_banks, act, turned, y_bf16 = {}, {}, {}, {}
+        x_words, w_grouped, w_codes, w_scales = {}, {}, {}, {}
+        h_banks, clamped, turned, y_bf16 = {}, {}, {}, {}
 
         def widen_x(h, i, on_vector):
+            row = x_raw_second[:, i, :] if h else x_raw_first[i][:]
             for c in range(PASSES):
                 wide = work.tile([P, GROUP], BF16, name="x_wide", bufs=PASSES * 2 * TILES)
-                x_wide[h, i, c] = (wide, on_vector)
-                for q in range(GROUP // XBLOCK):
-                    j = c * (GROUP // XBLOCK) + q
-                    row = x_raw_late[:, i, :] if h else x_raw[i][:]
-                    src = row[:, j * XBLOCK:(j + 1) * XBLOCK].bitcast(FP8)
-                    dst = wide[:, q * XBLOCK:(q + 1) * XBLOCK]
+                for q in range(GROUP // X_BLOCK):
+                    j = c * (GROUP // X_BLOCK) + q
+                    src = row[:, j * X_BLOCK:(j + 1) * X_BLOCK].bitcast(FP8)
                     scale = x_scale[h][:, i, j:j + 1]
                     if on_vector:
-                        dst = wide[:].rearrange("p (u q a e) -> p q a u e", u=2, q=4, e=2)[:, q]
+                        dst = wide[:].rearrange("p (u q a e) -> p q a u e", u=2, q=GROUP // X_BLOCK, e=2)[:, q]
                         nc.vector.tensor_scalar(out=dst, in0=src.rearrange("p (a u e) -> p a u e", u=2, e=2),
                                                 scalar1=scale, scalar2=None, op0=ALU.mult)
                     else:
-                        nc.scalar.activation(out=dst, in_=src, func=ACT.Copy, scale=scale)
-
-        def turn_x(h, i, on_vector=False):
-            pairs = x_grouped[h][:].rearrange("p c m t -> p c (m t)").bitcast(F32).rearrange("p c (m u) -> p c m u", u=2)
-            bank = psum.tile([P, GROUP], F32, name="turn")
-            for c in range(PASSES):
-                wide, is_sorted = x_wide[h, i, c]
+                        nc.scalar.activation(out=wide[:, q * X_BLOCK:(q + 1) * X_BLOCK], in_=src,
+                                             func=ACT.Copy, scale=scale)
                 words = wide[:].bitcast(F32)
                 for u in range(2):
+                    x_words[h, i, c, u] = words[:, u * P:(u + 1) * P] if on_vector else words[:, u:2 * P:2]
+
+        def turn_x(h, i):
+            bank = psum.tile([P, GROUP], F32, name="turn")
+            for c in range(PASSES):
+                for u in range(2):
                     col = (2 * c + u) * P
-                    src = words[:, u * P:(u + 1) * P] if is_sorted else words[:, u:GROUP // 2:2]
-                    nc.tensor.transpose(bank[:, col:col + P], src, ident[:])
-            copy = nc.vector.tensor_copy if on_vector else nc.scalar.copy
-            copy(out=pairs[:, :, i * P:(i + 1) * P, :], in_=bank[:].rearrange("p (c u m) -> p c m u", c=PASSES, u=2))
+                    nc.tensor.transpose(bank[:, col:col + P], x_words[h, i, c, u], ident[:])
+            pairs = x_grouped[h][:].rearrange("p c m j -> p c (m j)").bitcast(F32).rearrange("p c (m u) -> p c m u", u=2)
+            nc.scalar.copy(out=pairs[:, :, i * P:(i + 1) * P, :],
+                           in_=bank[:].rearrange("p (c u m) -> p c m u", c=PASSES, u=2))
 
         def quantize_x(h):
-            for run in (slice(0, 512), slice(512, PASSES * HALF)):
-                nc.vector.quantize_mx(out=x_codes[h][:].rearrange("p c m -> p (c m)")[:, run].bitcast(FP8X4),
-                                      scales=x_scales[h][:].rearrange("p c m -> p (c m)")[:, run],
-                                      in_=x_grouped[h][:].rearrange("p c m t -> p (c m) t")[:, run, :].rearrange("p m t -> p (m t)"))
+            codes = x_codes[h][:].rearrange("p c m -> p (c m)")
+            scales = x_scales[h][:].rearrange("p c m -> p (c m)")
+            values = x_grouped[h][:].rearrange("p c m j -> p (c m) j")
+            for run in (slice(0, GROUP), slice(GROUP, PASSES * HALF)):
+                nc.vector.quantize_mx(out=codes[:, run].bitcast(FP8X4), scales=scales[:, run],
+                                      in_=values[:, run, :].rearrange("p m j -> p (m j)"))
 
-        def interleave_w(n, split, helper):
-            head = n < PASSES
-            grouped = work.tile([P, PACK, P, PACK], BF16, name="w_head" if head else "w_grouped", bufs=2 if head else W_BUFS, align_bytes=64)
+        def interleave_w(n, gpsimd_share, scalar_share):
+            if n < PASSES:
+                grouped = work.tile([P, PACK, P, PACK], BF16, name="w_grouped_first", bufs=PASSES, align_bytes=64)
+            else:
+                grouped = work.tile([P, PACK, P, PACK], BF16, name="w_grouped", bufs=1, align_bytes=64)
             w_grouped[n] = grouped
-            if split and helper == "scalar":
-                nc.scalar.copy(out=grouped[:, :, :split, :].rearrange("p t (a i) j -> p a t i j", i=2),
-                               in_=w_raw[n][:, :, :PACK * split].rearrange("p j (a i t) -> p a t i j", i=2, t=PACK))
-            elif split:
-                nc.gpsimd.tensor_scalar(out=grouped[:, :, :split, :].rearrange("p t m j -> p m t j"),
-                                        in0=w_raw[n][:, :, :PACK * split].rearrange("p j (m t) -> p m t j", t=PACK),
+            dst = grouped[:].rearrange("p t m j -> p m j t")
+            src = w_raw[n][:].rearrange("p j (m t) -> p m j t", t=PACK)
+            cut = gpsimd_share + scalar_share
+            if gpsimd_share:
+                nc.gpsimd.tensor_scalar(out=dst[:, :gpsimd_share].rearrange("p m j t -> p m t j"),
+                                        in0=src[:, :gpsimd_share].rearrange("p m j t -> p m t j"),
                                         scalar1=1.0, scalar2=0.0, op0=ALU.mult, op1=ALU.add)
-            nc.vector.tensor_copy(
-                out=grouped[:, :, split:, :].rearrange("p t m j -> p m j t"),
-                in_=w_raw[n][:, :, PACK * split:].rearrange("p j (m t) -> p m j t", t=PACK))
+            if scalar_share:
+                nc.scalar.copy(out=dst[:, gpsimd_share:cut], in_=src[:, gpsimd_share:cut])
+            nc.vector.tensor_copy(out=dst[:, cut:], in_=src[:, cut:])
 
         def quantize_w(n):
-            w_codes[n] = work.tile([P, GROUP], U32, name="w_codes", bufs=6, align_bytes=64)
-            w_scales[n] = work.tile([P, GROUP], U8, name="w_scales", bufs=6, align_bytes=64)
+            w_codes[n] = work.tile([P, GROUP], U32, name="w_codes", bufs=W_CODE_SLOTS, align_bytes=64)
+            w_scales[n] = work.tile([P, GROUP], U8, name="w_scales", bufs=W_CODE_SLOTS, align_bytes=64)
             nc.vector.quantize_mx(out=w_codes[n][:].bitcast(FP8X4), scales=w_scales[n][:],
                                   in_=w_grouped[n][:].rearrange("p t m j -> p (t m j)"))
 
@@ -150,112 +158,110 @@ def tile_squared_relu_up_projection_b1_kernel(tc, X_bytes, X_scale, W, b, out_0,
                                         rhs=x_codes[h][:, c, run].bitcast(FP8X4), rhs_scale=x_scales[h][:, c, run],
                                         start=(c == 0), stop=(c == PASSES - 1))
 
-        def rectify(step, t, on_vector):
+        def add_bias_and_clamp(step):
             g = step // 2
-            if t == 0:
-                act[step] = work.tile([P, PACK, HALF], F32, name="act")
-            src = h_banks[step, t][:, :HALF]
-            if on_vector:
-                nc.vector.tensor_scalar(out=act[step][:, t, :], in0=src, scalar1=bias[:, g, t:t + 1], scalar2=0.0,
-                                        op0=ALU.add, op1=ALU.max)
-            else:
-                nc.scalar.activation(out=act[step][:, t, :], in_=src, func=ACT.Relu, bias=bias[:, g, t:t + 1])
+            clamped[step] = work.tile([P, PACK, HALF], F32, name="clamped")
+            for t in range(PACK):
+                src, dst = h_banks[step, t][:, :HALF], clamped[step][:, t, :]
+                if step == 0:
+                    nc.scalar.activation(out=dst, in_=src, func=ACT.Relu, bias=bias[:, g, t:t + 1])
+                else:
+                    nc.vector.tensor_scalar(out=dst, in0=src, scalar1=bias[:, g, t:t + 1], scalar2=0.0,
+                                            op0=ALU.add, op1=ALU.max)
 
-        def turn_act(step, i):
+        def turn_clamped(step, i):
             bank = psum.tile([P, GROUP], F32, name="turn")
             turned[step, i] = bank
             for t in range(PACK):
-                nc.tensor.transpose(bank[:, t * P:(t + 1) * P], act[step][:, t, i * P:(i + 1) * P], ident[:])
+                nc.tensor.transpose(bank[:, t * P:(t + 1) * P], clamped[step][:, t, i * P:(i + 1) * P], ident[:])
 
         def square_for_planes(step):
             g, h = divmod(step, 2)
             if h == 0:
                 y_bf16[g] = work.tile([P, T, PACK], BF16, name="y_bf16", bufs=2, align_bytes=64)
             dst = y_bf16[g][:, h * HALF:(h + 1) * HALF, :].rearrange("p (a i) t -> p a t i", i=2)
-            src = act[step][:].rearrange("p t (a i) -> p a t i", i=2)
-            cut = (HALF - VECTOR_SQUARE[step]) // 2
-            if cut > 0:
+            src = clamped[step][:].rearrange("p t (a i) -> p a t i", i=2)
+            if step + W_AHEAD < W_TILES:
+                nc.scalar.activation(out=dst, in_=src, func=ACT.Square)
+            else:
+                cut = (HALF - (VECTOR_TOKENS_LAST if step == STEPS - 1 else VECTOR_TOKENS_LATE)) // 2
                 nc.scalar.activation(out=dst[:, :cut], in_=src[:, :cut], func=ACT.Square)
-            if cut < HALF // 2:
                 nc.vector.tensor_tensor(out=dst[:, cut:], in0=src[:, cut:], in1=src[:, cut:], op=ALU.mult)
 
         def square_and_store(step):
             g, h = divmod(step, 2)
-            y = work.tile([P, TILES, GROUP], F32, name="y", bufs=6)
+            y = work.tile([P, TILES, GROUP], F32, name="y", bufs=RESULT_SLOTS)
             dst = out_0[h * HALF:(h + 1) * HALF, g * GROUP:(g + 1) * GROUP].rearrange("(i p) f -> p i f", p=P)
             for i in range(TILES):
                 nc.scalar.activation(out=y[:, i, :].rearrange("p (m t) -> p m t", t=PACK),
                                      in_=turned[step, i][:].rearrange("p (t m) -> p m t", t=PACK), func=ACT.Square)
                 nc.sync.dma_start(out=dst[:, i, :], in_=y[:, i, :])
 
-        def store_scales(plane, g0, g1):
-            for quad in range(4):
-                dst = out_2[g0:g1, 4 * quad:4 * quad + 4, :].rearrange("g r m -> r g m")
-                nc.sync.dma_start(out=dst.bitcast(I32), in_=plane[32 * quad:32 * quad + 4, :, :].bitcast(I32))
+        def store_scales(plane, first_group, end_group):
+            for q in range(QUADRANTS):
+                dst = out_2[first_group:end_group, 4 * q:4 * q + 4, :].rearrange("g r m -> r g m")
+                nc.sync.dma_start(out=dst.bitcast(I32), in_=plane[32 * q:32 * q + 4, :, :].bitcast(I32))
 
         def quantize_y(step):
             g, h = divmod(step, 2)
             if g < GROUPS - 1:
-                runs = [(slice(0, 256), slice(256, T))[h]]
+                runs = [slice(RUNS[0].stop, T) if h else RUNS[0]]
             else:
                 runs = [slice(h * HALF + run.start, h * HALF + run.stop) for run in RUNS]
-            first, last = runs[0].start, runs[-1].stop
-            codes = work.tile([P, last - first], U32, name="y_codes", bufs=6, align_bytes=64)
-            plane = y_scales_last[:, g - EARLY_GROUPS, :] if g >= EARLY_GROUPS else y_scales_early[:, g, :]
+            first, end = runs[0].start, runs[-1].stop
+            codes = work.tile([P, end - first], U32, name="y_codes", bufs=RESULT_SLOTS, align_bytes=64)
+            plane = y_scales_early[:, g, :] if g < EARLY_GROUPS else y_scales_late[:, g - EARLY_GROUPS, :]
             for run in runs:
-                nc.vector.quantize_mx(out=codes[:, run.start - first:run.stop - first].bitcast(FP8X4), scales=plane[:, run],
-                                      in_=y_bf16[g][:, run, :].rearrange("p m t -> p (m t)"))
-            dst = out_1[g, :, first:last, :].rearrange("p m t -> p (m t)")
+                nc.vector.quantize_mx(out=codes[:, run.start - first:run.stop - first].bitcast(FP8X4),
+                                      scales=plane[:, run], in_=y_bf16[g][:, run, :].rearrange("p m t -> p (m t)"))
+            dst = out_1[g, :, first:end, :].rearrange("p m t -> p (m t)")
             nc.sync.dma_start(out=dst.bitcast(I32), in_=codes[:].bitcast(I32))
             if step == 2 * EARLY_GROUPS - 1:
                 store_scales(y_scales_early, 0, EARLY_GROUPS)
             if step == STEPS - 1:
-                store_scales(y_scales_last, EARLY_GROUPS, GROUPS)
+                store_scales(y_scales_late, EARLY_GROUPS, GROUPS)
 
-        widen_x(0, 0, True)
-        widen_x(0, 2, False)
-        widen_x(0, 1, True)
-        turn_x(0, 0)
-        interleave_w(0, HEAD_SPLIT[0], "scalar")
-        turn_x(0, 1)
-        turn_x(0, 2)
-        interleave_w(1, HEAD_SPLIT[1], "scalar")
+        widen_x(0, 0, on_vector=True)
+        widen_x(0, 2, on_vector=False)
+        widen_x(0, 1, on_vector=True)
+        interleave_w(0, 0, 0)
+        for i in range(TILES):
+            turn_x(0, i)
+        widen_x(1, 0, on_vector=False)
+        widen_x(1, 1, on_vector=False)
+        widen_x(1, 2, on_vector=True)
+        interleave_w(1, 0, 0)
         quantize_w(0)
         quantize_x(0)
         quantize_w(1)
+        for i in (0, 2, 1):
+            turn_x(1, i)
         for t in range(PACK):
             multiply(0, t)
-        widen_x(1, 0, False)
-        widen_x(1, 1, False)
-        interleave_w(2, 0, None)
-        widen_x(1, 2, True)
+        interleave_w(2, 0, HEAD_SCALAR_SHARE)
+        quantize_x(1)
         quantize_w(2)
-        turn_x(1, 0)
-        turn_x(1, 1)
-        turn_x(1, 2)
 
         for step in range(STEPS):
-            for t in range(PACK):
-                rectify(step, t, t < PACK - SCALAR_RELU[step])
+            add_bias_and_clamp(step)
             n = step + W_AHEAD
-            if step == 0:
-                quantize_x(1)
-            if n < GROUPS * PASSES:
-                interleave_w(n, GPSIMD_COLUMNS[step], "gpsimd")
+            if n < W_TILES:
+                interleave_w(n, GPSIMD_SHARE if step else 0, SCALAR_SHARE)
             if step > 0:
                 quantize_y(step - 1)
-            if n < GROUPS * PASSES:
+            if n < W_TILES:
                 quantize_w(n)
             if step < STEPS - 1:
-                for t in range(PACK - 1):
+                for t in range(PACK // 2):
                     multiply(step + 1, t)
-                turn_act(step, 0)
-                turn_act(step, 1)
-                multiply(step + 1, PACK - 1)
-                turn_act(step, 2)
+                for i in range(TILES - 1):
+                    turn_clamped(step, i)
+                for t in range(PACK // 2, PACK):
+                    multiply(step + 1, t)
+                turn_clamped(step, TILES - 1)
             else:
                 for i in range(TILES):
-                    turn_act(step, i)
+                    turn_clamped(step, i)
             square_for_planes(step)
             square_and_store(step)
         quantize_y(STEPS - 1)

@@ -31,13 +31,15 @@ QUADRANTS = 4
 
 W_AHEAD = 3
 GPSIMD_SHARE = 64
-SCALAR_SHARE = 4
-HEAD_SCALAR_SHARE = 32
-VECTOR_TOKENS_LATE = 96
-VECTOR_TOKENS_LAST = 256
-EARLY_GROUPS = GROUPS - 2
+HEAD_SCALAR_SHARE = 40
+VECTOR_TOKENS_LATE = 224
+VECTOR_TOKENS_LAST = 320
+PACKED = 4
 W_CODE_SLOTS = 3 * PASSES
 RESULT_SLOTS = 6
+STAGING_SLOTS = 3
+W_LOADS = ((1, 2), (2, 4), (4, 8))
+LAST_WHOLE_STORE = STEPS // 2 - 1
 
 
 def tile_squared_relu_up_projection_b1_kernel(tc, X_bytes, X_scale, W, b, out_0, out_1, out_2):
@@ -53,46 +55,52 @@ def tile_squared_relu_up_projection_b1_kernel(tc, X_bytes, X_scale, W, b, out_0,
 
         x_scale = [keep.tile([P, TILES, K // X_BLOCK], F32, name="x_scale%d" % h) for h in range(2)]
         bias = keep.tile([P, GROUPS, PACK], BF16, name="bias")
-        x_raw_first = [keep.tile([P, K], U8, name="x_raw_first%d" % i) for i in range(TILES)]
-        x_raw_second = keep.tile([P, TILES, K], U8, name="x_raw_second")
-        w_raw = [keep.tile([P, PACK, GROUP], BF16, name="w_raw%d" % n) for n in range(W_TILES)]
+        x_raw = [keep.tile([P, K], U8, name="x_raw%d" % i) for i in range(2 * TILES)]
+        w_raw = {}
         x_grouped = [keep.tile([P, PASSES, HALF, PACK], BF16, name="x_grouped%d" % h, align_bytes=64) for h in range(2)]
         x_codes = [keep.tile([P, PASSES, HALF], U32, name="x_codes%d" % h, align_bytes=64) for h in range(2)]
         x_scales = [keep.tile([P, PASSES, HALF], U8, name="x_scales%d" % h, align_bytes=64) for h in range(2)]
-        y_scales_early = keep.tile([P, EARLY_GROUPS, T], U8, name="y_scales_early", align_bytes=64)
-        y_scales_late = keep.tile([P, GROUPS - EARLY_GROUPS, T], U8, name="y_scales_late", align_bytes=64)
+        y_scales = [keep.tile([P, T], U8, name="y_scales%d" % a, align_bytes=64) for a in range(GROUPS // PACKED)]
 
         def load_x_scale(h, queue):
             rows = X_scale[h * HALF:(h + 1) * HALF, :]
             queue.dma_start(out=x_scale[h][:], in_=rows.rearrange("(i p) j -> p i j", p=P))
 
-        def load_w(n):
-            g, c = divmod(n, PASSES)
-            rows = W[c * GROUP:(c + 1) * GROUP, g * GROUP:(g + 1) * GROUP]
-            nc.sync.dma_start(out=w_raw[n][:], in_=rows.rearrange("(p j) n -> p j n", j=PACK))
+        def load_x(i):
+            nc.sync.dma_start(out=x_raw[i][:], in_=X_bytes[i * P:(i + 1) * P, :])
+
+        def load_w(first_group, end_group):
+            for c in range(PASSES):
+                width = (end_group - first_group) * GROUP
+                tile = keep.tile([P, PACK, width], BF16, name="w_raw%d_%d" % (first_group, c))
+                rows = W[c * GROUP:(c + 1) * GROUP, first_group * GROUP:end_group * GROUP]
+                nc.sync.dma_start(out=tile[:], in_=rows.rearrange("(p j) n -> p j n", j=PACK))
+                for g in range(first_group, end_group):
+                    w_raw[g * PASSES + c] = tile[:, :, (g - first_group) * GROUP:(g - first_group + 1) * GROUP]
 
         load_x_scale(0, nc.scalar)
-        for i in (0, 2, 1):
-            nc.sync.dma_start(out=x_raw_first[i][:], in_=X_bytes[i * P:(i + 1) * P, :])
-        load_w(0)
+        table_warm_up = keep.tile([P, 1], F32, name="table_warm_up")
+        nc.scalar.activation(out=table_warm_up[:], in_=ident[:, 0:1], func=ACT.Square)
+        for i in range(TILES):
+            load_x(i)
+        load_w(0, 1)
         load_x_scale(1, nc.sync)
-        nc.sync.dma_start(out=x_raw_second[:], in_=X_bytes[HALF:, :].rearrange("(i p) k -> p i k", p=P))
-        load_w(1)
+        for i in range(TILES, 2 * TILES):
+            load_x(i)
         nc.sync.dma_start(out=bias[:], in_=b.rearrange("o (g p t) -> p (o g) t", p=P, t=PACK))
-        for n in range(PASSES, W_TILES):
-            load_w(n)
+        for first_group, end_group in W_LOADS:
+            load_w(first_group, end_group)
 
         x_words, w_grouped, w_codes, w_scales = {}, {}, {}, {}
-        h_banks, clamped, turned, y_bf16 = {}, {}, {}, {}
+        h_banks, clamped, turned, y_bf16, y_codes, y_rows = {}, {}, {}, {}, {}, {}
 
-        def widen_x(h, i, on_vector):
-            row = x_raw_second[:, i, :] if h else x_raw_first[i][:]
+        def widen_x(i, on_vector):
             for c in range(PASSES):
                 wide = work.tile([P, GROUP], BF16, name="x_wide", bufs=PASSES * 2 * TILES)
                 for q in range(GROUP // X_BLOCK):
                     j = c * (GROUP // X_BLOCK) + q
-                    src = row[:, j * X_BLOCK:(j + 1) * X_BLOCK].bitcast(FP8)
-                    scale = x_scale[h][:, i, j:j + 1]
+                    src = x_raw[i][:, j * X_BLOCK:(j + 1) * X_BLOCK].bitcast(FP8)
+                    scale = x_scale[i // TILES][:, i % TILES, j:j + 1]
                     if on_vector:
                         dst = wide[:].rearrange("p (u q a e) -> p q a u e", u=2, q=GROUP // X_BLOCK, e=2)[:, q]
                         nc.vector.tensor_scalar(out=dst, in0=src.rearrange("p (a u e) -> p a u e", u=2, e=2),
@@ -102,17 +110,18 @@ def tile_squared_relu_up_projection_b1_kernel(tc, X_bytes, X_scale, W, b, out_0,
                                              func=ACT.Copy, scale=scale)
                 words = wide[:].bitcast(F32)
                 for u in range(2):
-                    x_words[h, i, c, u] = words[:, u * P:(u + 1) * P] if on_vector else words[:, u:2 * P:2]
+                    x_words[i, c, u] = words[:, u * P:(u + 1) * P] if on_vector else words[:, u:2 * P:2]
 
-        def turn_x(h, i):
+        def turn_x(i, on_vector=False):
+            h, first = i // TILES, i % TILES * P
             bank = psum.tile([P, GROUP], F32, name="turn")
             for c in range(PASSES):
                 for u in range(2):
                     col = (2 * c + u) * P
-                    nc.tensor.transpose(bank[:, col:col + P], x_words[h, i, c, u], ident[:])
+                    nc.tensor.transpose(bank[:, col:col + P], x_words[i, c, u], ident[:])
             pairs = x_grouped[h][:].rearrange("p c m j -> p c (m j)").bitcast(F32).rearrange("p c (m u) -> p c m u", u=2)
-            nc.scalar.copy(out=pairs[:, :, i * P:(i + 1) * P, :],
-                           in_=bank[:].rearrange("p (c u m) -> p c m u", c=PASSES, u=2))
+            copy = nc.vector.tensor_copy if on_vector else nc.scalar.copy
+            copy(out=pairs[:, :, first:first + P, :], in_=bank[:].rearrange("p (c u m) -> p c m u", c=PASSES, u=2))
 
         def quantize_x(h):
             codes = x_codes[h][:].rearrange("p c m -> p (c m)")
@@ -122,14 +131,14 @@ def tile_squared_relu_up_projection_b1_kernel(tc, X_bytes, X_scale, W, b, out_0,
                 nc.vector.quantize_mx(out=codes[:, run].bitcast(FP8X4), scales=scales[:, run],
                                       in_=values[:, run, :].rearrange("p m j -> p (m j)"))
 
-        def interleave_w(n, gpsimd_share, scalar_share):
+        def interleave_w(n, gpsimd_share=0, scalar_share=0):
             if n < PASSES:
-                grouped = work.tile([P, PACK, P, PACK], BF16, name="w_grouped_first", bufs=PASSES, align_bytes=64)
+                grouped = work.tile([P, PACK * GROUP], BF16, name="w_grouped_first", bufs=PASSES, align_bytes=64)
             else:
-                grouped = work.tile([P, PACK, P, PACK], BF16, name="w_grouped", bufs=1, align_bytes=64)
+                grouped = work.tile([P, PACK * GROUP], BF16, name="staging", bufs=STAGING_SLOTS, align_bytes=64)
             w_grouped[n] = grouped
-            dst = grouped[:].rearrange("p t m j -> p m j t")
-            src = w_raw[n][:].rearrange("p j (m t) -> p m j t", t=PACK)
+            dst = grouped[:].rearrange("p (t m j) -> p m j t", t=PACK, j=PACK)
+            src = w_raw[n].rearrange("p j (m t) -> p m j t", t=PACK)
             cut = gpsimd_share + scalar_share
             if gpsimd_share:
                 nc.gpsimd.tensor_scalar(out=dst[:, :gpsimd_share].rearrange("p m j t -> p m t j"),
@@ -142,8 +151,12 @@ def tile_squared_relu_up_projection_b1_kernel(tc, X_bytes, X_scale, W, b, out_0,
         def quantize_w(n):
             w_codes[n] = work.tile([P, GROUP], U32, name="w_codes", bufs=W_CODE_SLOTS, align_bytes=64)
             w_scales[n] = work.tile([P, GROUP], U8, name="w_scales", bufs=W_CODE_SLOTS, align_bytes=64)
-            nc.vector.quantize_mx(out=w_codes[n][:].bitcast(FP8X4), scales=w_scales[n][:],
-                                  in_=w_grouped[n][:].rearrange("p t m j -> p (t m j)"))
+            nc.vector.quantize_mx(out=w_codes[n][:].bitcast(FP8X4), scales=w_scales[n][:], in_=w_grouped[n][:])
+
+        def warm_up_tensor_engine(operand, columns, count):
+            bank = psum.tile([P, GROUP], F32, name="h")
+            for r in range(count):
+                nc.tensor.matmul(bank[:, :columns], lhsT=operand[:, :P], rhs=operand[:, :columns], start=True, stop=True)
 
         def multiply(step, t):
             g, h = divmod(step, 2)
@@ -158,16 +171,17 @@ def tile_squared_relu_up_projection_b1_kernel(tc, X_bytes, X_scale, W, b, out_0,
                                         rhs=x_codes[h][:, c, run].bitcast(FP8X4), rhs_scale=x_scales[h][:, c, run],
                                         start=(c == 0), stop=(c == PASSES - 1))
 
-        def add_bias_and_clamp(step):
+        def add_bias_and_clamp(step, slices, on_vector):
             g = step // 2
-            clamped[step] = work.tile([P, PACK, HALF], F32, name="clamped")
-            for t in range(PACK):
+            if step not in clamped:
+                clamped[step] = work.tile([P, PACK, HALF], F32, name="clamped")
+            for t in slices:
                 src, dst = h_banks[step, t][:, :HALF], clamped[step][:, t, :]
-                if step == 0:
-                    nc.scalar.activation(out=dst, in_=src, func=ACT.Relu, bias=bias[:, g, t:t + 1])
-                else:
+                if on_vector:
                     nc.vector.tensor_scalar(out=dst, in0=src, scalar1=bias[:, g, t:t + 1], scalar2=0.0,
                                             op0=ALU.add, op1=ALU.max)
+                else:
+                    nc.scalar.activation(out=dst, in_=src, func=ACT.Relu, bias=bias[:, g, t:t + 1])
 
         def turn_clamped(step, i):
             bank = psum.tile([P, GROUP], F32, name="turn")
@@ -175,93 +189,120 @@ def tile_squared_relu_up_projection_b1_kernel(tc, X_bytes, X_scale, W, b, out_0,
             for t in range(PACK):
                 nc.tensor.transpose(bank[:, t * P:(t + 1) * P], clamped[step][:, t, i * P:(i + 1) * P], ident[:])
 
-        def square_for_planes(step):
-            g, h = divmod(step, 2)
-            if h == 0:
-                y_bf16[g] = work.tile([P, T, PACK], BF16, name="y_bf16", bufs=2, align_bytes=64)
-            dst = y_bf16[g][:, h * HALF:(h + 1) * HALF, :].rearrange("p (a i) t -> p a t i", i=2)
+        def plane_views(step):
+            dst = y_bf16[step][:, :HALF * PACK].rearrange("p (a i t) -> p a t i", i=2, t=PACK)
             src = clamped[step][:].rearrange("p t (a i) -> p a t i", i=2)
+            return dst, src
+
+        def vector_tokens(step):
             if step + W_AHEAD < W_TILES:
-                nc.scalar.activation(out=dst, in_=src, func=ACT.Square)
-            else:
-                cut = (HALF - (VECTOR_TOKENS_LAST if step == STEPS - 1 else VECTOR_TOKENS_LATE)) // 2
-                nc.scalar.activation(out=dst[:, :cut], in_=src[:, :cut], func=ACT.Square)
+                return 0
+            return VECTOR_TOKENS_LAST if step == STEPS - 1 else VECTOR_TOKENS_LATE
+
+        def square_for_planes(step):
+            y_bf16[step] = work.tile([P, PACK * GROUP], BF16, name="staging", bufs=STAGING_SLOTS, align_bytes=64)
+            dst, src = plane_views(step)
+            cut = (HALF - vector_tokens(step)) // 2
+            nc.scalar.activation(out=dst[:, :cut], in_=src[:, :cut], func=ACT.Square)
+            if vector_tokens(step):
                 nc.vector.tensor_tensor(out=dst[:, cut:], in0=src[:, cut:], in1=src[:, cut:], op=ALU.mult)
 
-        def square_and_store(step):
+        def square_and_store(step, i, queue):
             g, h = divmod(step, 2)
-            y = work.tile([P, TILES, GROUP], F32, name="y", bufs=RESULT_SLOTS)
+            if i == 0:
+                y_rows[step] = work.tile([P, TILES, GROUP], F32, name="y", bufs=RESULT_SLOTS)
+            y = y_rows[step]
+            nc.scalar.activation(out=y[:, i, :].rearrange("p (m t) -> p m t", t=PACK),
+                                 in_=turned[step, i][:].rearrange("p (t m) -> p m t", t=PACK), func=ACT.Square)
             dst = out_0[h * HALF:(h + 1) * HALF, g * GROUP:(g + 1) * GROUP].rearrange("(i p) f -> p i f", p=P)
-            for i in range(TILES):
-                nc.scalar.activation(out=y[:, i, :].rearrange("p (m t) -> p m t", t=PACK),
-                                     in_=turned[step, i][:].rearrange("p (t m) -> p m t", t=PACK), func=ACT.Square)
-                nc.sync.dma_start(out=dst[:, i, :], in_=y[:, i, :])
+            if step > LAST_WHOLE_STORE:
+                queue.dma_start(out=dst[:, i, :], in_=y[:, i, :])
+            elif i == TILES - 1:
+                queue.dma_start(out=dst, in_=y[:])
 
-        def store_scales(plane, first_group, end_group):
+        def store_scales(a):
             for q in range(QUADRANTS):
-                dst = out_2[first_group:end_group, 4 * q:4 * q + 4, :].rearrange("g r m -> r g m")
-                nc.sync.dma_start(out=dst.bitcast(I32), in_=plane[32 * q:32 * q + 4, :, :].bitcast(I32))
+                dst = out_2[a * PACKED:(a + 1) * PACKED, 4 * q:4 * q + 4, :]
+                nc.sync.dma_start(out=dst.bitcast(I32), in_=y_scales[a][32 * q:32 * q + 4 * PACKED, :].bitcast(I32))
 
         def quantize_y(step):
             g, h = divmod(step, 2)
-            if g < GROUPS - 1:
-                runs = [slice(RUNS[0].stop, T) if h else RUNS[0]]
-            else:
-                runs = [slice(h * HALF + run.start, h * HALF + run.stop) for run in RUNS]
-            first, end = runs[0].start, runs[-1].stop
-            codes = work.tile([P, end - first], U32, name="y_codes", bufs=RESULT_SLOTS, align_bytes=64)
-            plane = y_scales_early[:, g, :] if g < EARLY_GROUPS else y_scales_late[:, g - EARLY_GROUPS, :]
-            for run in runs:
-                nc.vector.quantize_mx(out=codes[:, run.start - first:run.stop - first].bitcast(FP8X4),
-                                      scales=plane[:, run], in_=y_bf16[g][:, run, :].rearrange("p m t -> p (m t)"))
-            dst = out_1[g, :, first:end, :].rearrange("p m t -> p (m t)")
-            nc.sync.dma_start(out=dst.bitcast(I32), in_=codes[:].bitcast(I32))
-            if step == 2 * EARLY_GROUPS - 1:
-                store_scales(y_scales_early, 0, EARLY_GROUPS)
-            if step == STEPS - 1:
-                store_scales(y_scales_late, EARLY_GROUPS, GROUPS)
+            if h == 0:
+                y_codes[g] = work.tile([P, T], U32, name="y_codes", bufs=RESULT_SLOTS // 2, align_bytes=64)
+            plane = y_scales[g // PACKED][4 * (g % PACKED):, :]
+            for run in RUNS:
+                tokens = slice(h * HALF + run.start, h * HALF + run.stop)
+                nc.vector.quantize_mx(out=y_codes[g][:, tokens].bitcast(FP8X4), scales=plane[:, tokens],
+                                      in_=y_bf16[step][:, run.start * PACK:run.stop * PACK])
 
-        widen_x(0, 0, on_vector=True)
-        widen_x(0, 2, on_vector=False)
-        widen_x(0, 1, on_vector=True)
-        interleave_w(0, 0, 0)
-        for i in range(TILES):
-            turn_x(0, i)
-        widen_x(1, 0, on_vector=False)
-        widen_x(1, 1, on_vector=False)
-        widen_x(1, 2, on_vector=True)
-        interleave_w(1, 0, 0)
+        def store_planes(step):
+            g, h = divmod(step, 2)
+            if g == GROUPS - 1 or h == 1:
+                tokens = slice(h * HALF, (h + 1) * HALF) if g == GROUPS - 1 else slice(0, T)
+                dst = out_1[g, :, tokens, :].rearrange("p m t -> p (m t)")
+                nc.sync.dma_start(out=dst.bitcast(I32), in_=y_codes[g][:, tokens].bitcast(I32))
+            if h == 1 and g % PACKED == PACKED - 1:
+                store_scales(g // PACKED)
+
+        widen_x(0, on_vector=True)
+        widen_x(1, on_vector=False)
+        widen_x(2, on_vector=True)
+        interleave_w(0)
+        turn_x(0)
+        turn_x(2)
+        turn_x(1)
+        warm_up_tensor_engine(w_grouped[0], GROUP, 4)
+        interleave_w(1, scalar_share=HEAD_SCALAR_SHARE)
         quantize_w(0)
         quantize_x(0)
         quantize_w(1)
-        for i in (0, 2, 1):
-            turn_x(1, i)
-        for t in range(PACK):
-            multiply(0, t)
-        interleave_w(2, 0, HEAD_SCALAR_SHARE)
+        widen_x(3, on_vector=False)
+        widen_x(4, on_vector=False)
+        widen_x(5, on_vector=True)
+        turn_x(3)
+        multiply(0, 0)
+        multiply(0, 1)
+        turn_x(5)
+        turn_x(4)
+        multiply(0, 2)
+        multiply(0, 3)
+        add_bias_and_clamp(0, range(PACK), on_vector=False)
+        interleave_w(2)
+        interleave_w(3)
         quantize_x(1)
         quantize_w(2)
-
+        quantize_w(3)
         for step in range(STEPS):
-            add_bias_and_clamp(step)
             n = step + W_AHEAD
-            if n < W_TILES:
-                interleave_w(n, GPSIMD_SHARE if step else 0, SCALAR_SHARE)
             if step > 0:
+                add_bias_and_clamp(step, range(PACK), on_vector=True)
+                if n < W_TILES:
+                    interleave_w(n, gpsimd_share=GPSIMD_SHARE)
                 quantize_y(step - 1)
-            if n < W_TILES:
-                quantize_w(n)
-            if step < STEPS - 1:
-                for t in range(PACK // 2):
+                store_planes(step - 1)
+                if n < W_TILES:
+                    quantize_w(n)
+            last = step == STEPS - 1
+            for t in range(PACK // 2):
+                if not last:
                     multiply(step + 1, t)
+            if step > 0:
+                turn_clamped(step - 1, TILES - 1)
+            else:
                 for i in range(TILES - 1):
                     turn_clamped(step, i)
-                for t in range(PACK // 2, PACK):
+            for t in range(PACK // 2, PACK):
+                if not last:
                     multiply(step + 1, t)
-                turn_clamped(step, TILES - 1)
-            else:
-                for i in range(TILES):
+            for i in range(TILES - 1):
+                if step > 0:
                     turn_clamped(step, i)
             square_for_planes(step)
-            square_and_store(step)
+            if step > 0:
+                square_and_store(step - 1, TILES - 1, nc.sync)
+            for i in range(TILES - 1):
+                square_and_store(step, i, nc.sync)
+        turn_clamped(STEPS - 1, TILES - 1)
         quantize_y(STEPS - 1)
+        store_planes(STEPS - 1)
+        square_and_store(STEPS - 1, TILES - 1, nc.scalar)

@@ -21,7 +21,8 @@ PACK = 4
 GROUP = P * PACK
 PASSES = K // GROUP
 GROUPS = F // GROUP
-W_TILES = GROUPS * PASSES
+UNITS = 2 * GROUPS
+UNIT_PART = 2 * P * PACK
 HALF = T // 2
 TILES = HALF // P
 STEPS = 2 * GROUPS
@@ -29,15 +30,13 @@ RUNS = (slice(0, 256), slice(256, HALF))
 X_BLOCK = 128
 QUADRANTS = 4
 
-W_AHEAD = 3
-GPSIMD_SHARE = 64
-HEAD_SCALAR_SHARE = 40
-VECTOR_TOKENS_LATE = 224
-VECTOR_TOKENS_LAST = 320
+W_AHEAD = 2
+VECTOR_TOKENS = (128, 192, 192)
+GPSIMD_TOKENS = 96
 PACKED = 4
-W_CODE_SLOTS = 3 * PASSES
+W_CODE_SLOTS = 6
 RESULT_SLOTS = 6
-STAGING_SLOTS = 3
+SLOTS = {"staging": 3, "w_vector": 2, "w_first": 4}
 W_LOADS = ((1, 2), (2, 4), (4, 8))
 LAST_WHOLE_STORE = STEPS // 2 - 1
 
@@ -112,7 +111,7 @@ def tile_squared_relu_up_projection_b1_kernel(tc, X_bytes, X_scale, W, b, out_0,
                 for u in range(2):
                     x_words[i, c, u] = words[:, u * P:(u + 1) * P] if on_vector else words[:, u:2 * P:2]
 
-        def turn_x(i, on_vector=False):
+        def turn_x(i):
             h, first = i // TILES, i % TILES * P
             bank = psum.tile([P, GROUP], F32, name="turn")
             for c in range(PASSES):
@@ -120,8 +119,8 @@ def tile_squared_relu_up_projection_b1_kernel(tc, X_bytes, X_scale, W, b, out_0,
                     col = (2 * c + u) * P
                     nc.tensor.transpose(bank[:, col:col + P], x_words[i, c, u], ident[:])
             pairs = x_grouped[h][:].rearrange("p c m j -> p c (m j)").bitcast(F32).rearrange("p c (m u) -> p c m u", u=2)
-            copy = nc.vector.tensor_copy if on_vector else nc.scalar.copy
-            copy(out=pairs[:, :, first:first + P, :], in_=bank[:].rearrange("p (c u m) -> p c m u", c=PASSES, u=2))
+            nc.scalar.copy(out=pairs[:, :, first:first + P, :],
+                           in_=bank[:].rearrange("p (c u m) -> p c m u", c=PASSES, u=2))
 
         def quantize_x(h):
             codes = x_codes[h][:].rearrange("p c m -> p (c m)")
@@ -131,27 +130,26 @@ def tile_squared_relu_up_projection_b1_kernel(tc, X_bytes, X_scale, W, b, out_0,
                 nc.vector.quantize_mx(out=codes[:, run].bitcast(FP8X4), scales=scales[:, run],
                                       in_=values[:, run, :].rearrange("p m j -> p (m j)"))
 
-        def interleave_w(n, gpsimd_share=0, scalar_share=0):
-            if n < PASSES:
-                grouped = work.tile([P, PACK * GROUP], BF16, name="w_grouped_first", bufs=PASSES, align_bytes=64)
-            else:
-                grouped = work.tile([P, PACK * GROUP], BF16, name="staging", bufs=STAGING_SLOTS, align_bytes=64)
-            w_grouped[n] = grouped
-            dst = grouped[:].rearrange("p (t m j) -> p m j t", t=PACK, j=PACK)
-            src = w_raw[n].rearrange("p j (m t) -> p m j t", t=PACK)
-            cut = gpsimd_share + scalar_share
-            if gpsimd_share:
-                nc.gpsimd.tensor_scalar(out=dst[:, :gpsimd_share].rearrange("p m j t -> p m t j"),
-                                        in0=src[:, :gpsimd_share].rearrange("p m j t -> p m t j"),
+        def interleave_w(n, c, engine, tag):
+            w_grouped[n, c] = work.tile([P, UNIT_PART], BF16, name=tag, bufs=SLOTS[tag], align_bytes=64)
+            g, v = divmod(n, 2)
+            dst = w_grouped[n, c][:].rearrange("p (e m j) -> p m j e", e=2, j=PACK)
+            src = w_raw[g * PASSES + c].rearrange("p j (m v e) -> p v m j e", v=2, e=2)[:, v]
+            if engine == "gpsimd":
+                nc.gpsimd.tensor_scalar(out=dst.rearrange("p m j e -> p m e j"), in0=src.rearrange("p m j e -> p m e j"),
                                         scalar1=1.0, scalar2=0.0, op0=ALU.mult, op1=ALU.add)
-            if scalar_share:
-                nc.scalar.copy(out=dst[:, gpsimd_share:cut], in_=src[:, gpsimd_share:cut])
-            nc.vector.tensor_copy(out=dst[:, cut:], in_=src[:, cut:])
+            elif engine == "scalar":
+                nc.scalar.copy(out=dst, in_=src)
+            else:
+                nc.vector.tensor_copy(out=dst, in_=src)
 
-        def quantize_w(n):
-            w_codes[n] = work.tile([P, GROUP], U32, name="w_codes", bufs=W_CODE_SLOTS, align_bytes=64)
-            w_scales[n] = work.tile([P, GROUP], U8, name="w_scales", bufs=W_CODE_SLOTS, align_bytes=64)
-            nc.vector.quantize_mx(out=w_codes[n][:].bitcast(FP8X4), scales=w_scales[n][:], in_=w_grouped[n][:])
+        def quantize_w(n, c):
+            if n not in w_codes:
+                w_codes[n] = work.tile([P, GROUP], U32, name="w_codes", bufs=W_CODE_SLOTS, align_bytes=64)
+                w_scales[n] = work.tile([P, GROUP], U8, name="w_scales", bufs=W_CODE_SLOTS, align_bytes=64)
+            cols = slice(c * 2 * P, (c + 1) * 2 * P)
+            nc.vector.quantize_mx(out=w_codes[n][:, cols].bitcast(FP8X4), scales=w_scales[n][:, cols],
+                                  in_=w_grouped[n, c][:])
 
         def warm_up_tensor_engine(operand, columns, count):
             bank = psum.tile([P, GROUP], F32, name="h")
@@ -162,21 +160,21 @@ def tile_squared_relu_up_projection_b1_kernel(tc, X_bytes, X_scale, W, b, out_0,
             g, h = divmod(step, 2)
             bank = psum.tile([P, GROUP], F32, name="h")
             h_banks[step, t] = bank
-            cols = slice(t * P, (t + 1) * P)
+            n = 2 * g + t // 2
             for run in RUNS:
                 for c in range(PASSES):
-                    n = g * PASSES + c
+                    cols = slice((2 * c + t % 2) * P, (2 * c + t % 2 + 1) * P)
                     nc.tensor.matmul_mx(out=bank[:, run],
                                         lhsT=w_codes[n][:, cols].bitcast(FP8X4), lhsT_scale=w_scales[n][:, cols],
                                         rhs=x_codes[h][:, c, run].bitcast(FP8X4), rhs_scale=x_scales[h][:, c, run],
                                         start=(c == 0), stop=(c == PASSES - 1))
 
-        def add_bias_and_clamp(step, slices, on_vector):
+        def add_bias_and_clamp(step, slices, on_vector, tokens=slice(0, HALF)):
             g = step // 2
             if step not in clamped:
                 clamped[step] = work.tile([P, PACK, HALF], F32, name="clamped")
             for t in slices:
-                src, dst = h_banks[step, t][:, :HALF], clamped[step][:, t, :]
+                src, dst = h_banks[step, t][:, tokens], clamped[step][:, t, tokens]
                 if on_vector:
                     nc.vector.tensor_scalar(out=dst, in0=src, scalar1=bias[:, g, t:t + 1], scalar2=0.0,
                                             op0=ALU.add, op1=ALU.max)
@@ -189,23 +187,28 @@ def tile_squared_relu_up_projection_b1_kernel(tc, X_bytes, X_scale, W, b, out_0,
             for t in range(PACK):
                 nc.tensor.transpose(bank[:, t * P:(t + 1) * P], clamped[step][:, t, i * P:(i + 1) * P], ident[:])
 
-        def plane_views(step):
-            dst = y_bf16[step][:, :HALF * PACK].rearrange("p (a i t) -> p a t i", i=2, t=PACK)
-            src = clamped[step][:].rearrange("p t (a i) -> p a t i", i=2)
+        def plane_views(tile, step, first, end):
+            dst = tile[:, first * PACK:end * PACK].rearrange("p (a i t) -> p a t i", i=2, t=PACK)
+            src = clamped[step][:, :, first:end].rearrange("p t (a i) -> p a t i", i=2)
             return dst, src
 
         def vector_tokens(step):
-            if step + W_AHEAD < W_TILES:
+            if step + 1 + W_AHEAD < UNITS:
                 return 0
-            return VECTOR_TOKENS_LAST if step == STEPS - 1 else VECTOR_TOKENS_LATE
+            return VECTOR_TOKENS[step - STEPS]
 
-        def square_for_planes(step):
-            y_bf16[step] = work.tile([P, PACK * GROUP], BF16, name="staging", bufs=STAGING_SLOTS, align_bytes=64)
-            dst, src = plane_views(step)
-            cut = (HALF - vector_tokens(step)) // 2
-            nc.scalar.activation(out=dst[:, :cut], in_=src[:, :cut], func=ACT.Square)
-            if vector_tokens(step):
-                nc.vector.tensor_tensor(out=dst[:, cut:], in0=src[:, cut:], in1=src[:, cut:], op=ALU.mult)
+        def square_for_planes(step, engine, first, end):
+            if step not in y_bf16:
+                y_bf16[step] = work.tile([P, PACK * HALF], BF16, name="staging", bufs=SLOTS["staging"], align_bytes=64)
+            dst, src = plane_views(y_bf16[step], step, first, end)
+            if engine == "scalar":
+                nc.scalar.activation(out=dst, in_=src, func=ACT.Square)
+            elif engine == "vector":
+                nc.vector.tensor_tensor(out=dst, in0=src, in1=src, op=ALU.mult)
+            else:
+                dst = y_bf16[step][:, first * PACK:end * PACK].rearrange("p (m t) -> p m t", t=PACK)
+                src = clamped[step][:, :, first:end].rearrange("p t m -> p m t")
+                nc.gpsimd.tensor_tensor(out=dst, in0=src, in1=src, op=ALU.mult)
 
         def square_and_store(step, i, queue):
             g, h = divmod(step, 2)
@@ -225,12 +228,12 @@ def tile_squared_relu_up_projection_b1_kernel(tc, X_bytes, X_scale, W, b, out_0,
                 dst = out_2[a * PACKED:(a + 1) * PACKED, 4 * q:4 * q + 4, :]
                 nc.sync.dma_start(out=dst.bitcast(I32), in_=y_scales[a][32 * q:32 * q + 4 * PACKED, :].bitcast(I32))
 
-        def quantize_y(step):
+        def quantize_y(step, runs):
             g, h = divmod(step, 2)
-            if h == 0:
+            if g not in y_codes:
                 y_codes[g] = work.tile([P, T], U32, name="y_codes", bufs=RESULT_SLOTS // 2, align_bytes=64)
             plane = y_scales[g // PACKED][4 * (g % PACKED):, :]
-            for run in RUNS:
+            for run in runs:
                 tokens = slice(h * HALF + run.start, h * HALF + run.stop)
                 nc.vector.quantize_mx(out=y_codes[g][:, tokens].bitcast(FP8X4), scales=plane[:, tokens],
                                       in_=y_bf16[step][:, run.start * PACK:run.stop * PACK])
@@ -247,62 +250,77 @@ def tile_squared_relu_up_projection_b1_kernel(tc, X_bytes, X_scale, W, b, out_0,
         widen_x(0, on_vector=True)
         widen_x(1, on_vector=False)
         widen_x(2, on_vector=True)
-        interleave_w(0)
+        interleave_w(0, 0, "vector", "w_first")
+        interleave_w(1, 0, "vector", "w_first")
         turn_x(0)
         turn_x(2)
         turn_x(1)
-        warm_up_tensor_engine(w_grouped[0], GROUP, 4)
-        interleave_w(1, scalar_share=HEAD_SCALAR_SHARE)
-        quantize_w(0)
+        warm_up_tensor_engine(w_grouped[0, 0], GROUP, 4)
+        interleave_w(0, 1, "vector", "w_first")
+        interleave_w(1, 1, "scalar", "w_first")
+        quantize_w(0, 0)
         quantize_x(0)
-        quantize_w(1)
+        quantize_w(0, 1)
         widen_x(3, on_vector=False)
-        widen_x(4, on_vector=False)
+        widen_x(4, on_vector=True)
         widen_x(5, on_vector=True)
-        turn_x(3)
+        quantize_w(1, 0)
+        quantize_w(1, 1)
         multiply(0, 0)
         multiply(0, 1)
-        turn_x(5)
+        add_bias_and_clamp(0, (0,), on_vector=False)
         turn_x(4)
+        turn_x(3)
+        turn_x(5)
         multiply(0, 2)
         multiply(0, 3)
-        add_bias_and_clamp(0, range(PACK), on_vector=False)
-        interleave_w(2)
-        interleave_w(3)
+        add_bias_and_clamp(0, (1, 2, 3), on_vector=False)
+        interleave_w(2, 0, "vector", "staging")
+        interleave_w(2, 1, "vector", "staging")
         quantize_x(1)
-        quantize_w(2)
-        quantize_w(3)
+        quantize_w(2, 1)
+        quantize_w(2, 0)
+        interleave_w(3, 1, "vector", "w_vector")
+
         for step in range(STEPS):
             n = step + W_AHEAD
-            if step > 0:
-                add_bias_and_clamp(step, range(PACK), on_vector=True)
-                if n < W_TILES:
-                    interleave_w(n, gpsimd_share=GPSIMD_SHARE)
-                quantize_y(step - 1)
-                store_planes(step - 1)
-                if n < W_TILES:
-                    quantize_w(n)
             last = step == STEPS - 1
+            if last:
+                for i in range(TILES):
+                    add_bias_and_clamp(step, range(PACK), on_vector=True, tokens=slice(i * P, (i + 1) * P))
+                    if i == 0:
+                        square_for_planes(step, "gpsimd", 0, GPSIMD_TOKENS)
+                quantize_y(step - 1, RUNS[:1])
+            elif step > 0:
+                add_bias_and_clamp(step, range(PACK), on_vector=True)
+                if n < UNITS:
+                    interleave_w(n, 0, "gpsimd", "staging")
+                    quantize_w(n, 1)
+                    quantize_w(n, 0)
+                quantize_y(step - 1, RUNS)
+                store_planes(step - 1)
+                if n + 1 < UNITS:
+                    interleave_w(n + 1, 1, "vector", "w_vector")
+            tiles_between = TILES - 1 if step else 0
             for t in range(PACK // 2):
                 if not last:
                     multiply(step + 1, t)
-            if step > 0:
-                turn_clamped(step - 1, TILES - 1)
-            else:
-                for i in range(TILES - 1):
-                    turn_clamped(step, i)
+            for i in range(tiles_between):
+                turn_clamped(step, i)
             for t in range(PACK // 2, PACK):
                 if not last:
                     multiply(step + 1, t)
-            for i in range(TILES - 1):
-                if step > 0:
-                    turn_clamped(step, i)
-            square_for_planes(step)
-            if step > 0:
-                square_and_store(step - 1, TILES - 1, nc.sync)
-            for i in range(TILES - 1):
+            for i in range(tiles_between, TILES):
+                turn_clamped(step, i)
+            first = GPSIMD_TOKENS if last else 0
+            cut = HALF - vector_tokens(step)
+            square_for_planes(step, "scalar", first, cut)
+            if cut < HALF:
+                square_for_planes(step, "vector", cut, HALF)
+            for i in range(TILES - 1 if last else TILES):
                 square_and_store(step, i, nc.sync)
-        turn_clamped(STEPS - 1, TILES - 1)
-        quantize_y(STEPS - 1)
+        quantize_y(STEPS - 2, RUNS[1:])
+        store_planes(STEPS - 2)
+        quantize_y(STEPS - 1, RUNS)
         store_planes(STEPS - 1)
         square_and_store(STEPS - 1, TILES - 1, nc.scalar)

@@ -31,8 +31,7 @@ X_BLOCK = 128
 QUADRANTS = 4
 
 W_AHEAD = 2
-VECTOR_TOKENS = (128, 192, 192)
-GPSIMD_TOKENS = 96
+VECTOR_TOKENS = (128, 192, 256)
 PACKED = 4
 W_CODE_SLOTS = 6
 RESULT_SLOTS = 6
@@ -203,12 +202,8 @@ def tile_squared_relu_up_projection_b1_kernel(tc, X_bytes, X_scale, W, b, out_0,
             dst, src = plane_views(y_bf16[step], step, first, end)
             if engine == "scalar":
                 nc.scalar.activation(out=dst, in_=src, func=ACT.Square)
-            elif engine == "vector":
-                nc.vector.tensor_tensor(out=dst, in0=src, in1=src, op=ALU.mult)
             else:
-                dst = y_bf16[step][:, first * PACK:end * PACK].rearrange("p (m t) -> p m t", t=PACK)
-                src = clamped[step][:, :, first:end].rearrange("p t m -> p m t")
-                nc.gpsimd.tensor_tensor(out=dst, in0=src, in1=src, op=ALU.mult)
+                nc.vector.tensor_tensor(out=dst, in0=src, in1=src, op=ALU.mult)
 
         def square_and_store(step, i, queue):
             g, h = divmod(step, 2)
@@ -288,8 +283,6 @@ def tile_squared_relu_up_projection_b1_kernel(tc, X_bytes, X_scale, W, b, out_0,
             if last:
                 for i in range(TILES):
                     add_bias_and_clamp(step, range(PACK), on_vector=True, tokens=slice(i * P, (i + 1) * P))
-                    if i == 0:
-                        square_for_planes(step, "gpsimd", 0, GPSIMD_TOKENS)
                 quantize_y(step - 1, RUNS[:1])
             elif step > 0:
                 add_bias_and_clamp(step, range(PACK), on_vector=True)
@@ -312,9 +305,8 @@ def tile_squared_relu_up_projection_b1_kernel(tc, X_bytes, X_scale, W, b, out_0,
                     multiply(step + 1, t)
             for i in range(tiles_between, TILES):
                 turn_clamped(step, i)
-            first = GPSIMD_TOKENS if last else 0
             cut = HALF - vector_tokens(step)
-            square_for_planes(step, "scalar", first, cut)
+            square_for_planes(step, "scalar", 0, cut)
             if cut < HALF:
                 square_for_planes(step, "vector", cut, HALF)
             for i in range(TILES - 1 if last else TILES):

@@ -35,7 +35,6 @@ VECTOR_TOKENS = (128, 192, 256)
 PACKED = 4
 W_CODE_SLOTS = 6
 RESULT_SLOTS = 6
-SLOTS = {"staging": 3, "w_vector": 2, "w_first": 4}
 W_LOADS = ((1, 2), (2, 4), (4, 8))
 LAST_WHOLE_STORE = STEPS // 2 - 1
 
@@ -58,6 +57,8 @@ def tile_squared_relu_up_projection_b1_kernel(tc, X_bytes, X_scale, W, b, out_0,
         x_grouped = [keep.tile([P, PASSES, HALF, PACK], BF16, name="x_grouped%d" % h, align_bytes=64) for h in range(2)]
         x_codes = [keep.tile([P, PASSES, HALF], U32, name="x_codes%d" % h, align_bytes=64) for h in range(2)]
         x_scales = [keep.tile([P, PASSES, HALF], U8, name="x_scales%d" % h, align_bytes=64) for h in range(2)]
+        w_first = [keep.tile([P, PASSES * UNIT_PART], BF16, name="w_first%d" % n, align_bytes=64) for n in range(W_AHEAD)]
+        w_shared = keep.tile([P, 3 * UNIT_PART], BF16, name="w_shared", align_bytes=64)
         y_scales = [keep.tile([P, T], U8, name="y_scales%d" % a, align_bytes=64) for a in range(GROUPS // PACKED)]
 
         def load_x_scale(h, queue):
@@ -89,7 +90,7 @@ def tile_squared_relu_up_projection_b1_kernel(tc, X_bytes, X_scale, W, b, out_0,
         for first_group, end_group in W_LOADS:
             load_w(first_group, end_group)
 
-        x_words, w_grouped, w_codes, w_scales = {}, {}, {}, {}
+        x_words, w_codes, w_scales = {}, {}, {}
         h_banks, clamped, turned, y_bf16, y_codes, y_rows = {}, {}, {}, {}, {}, {}
 
         def widen_x(i, on_vector):
@@ -129,10 +130,18 @@ def tile_squared_relu_up_projection_b1_kernel(tc, X_bytes, X_scale, W, b, out_0,
                 nc.vector.quantize_mx(out=codes[:, run].bitcast(FP8X4), scales=scales[:, run],
                                       in_=values[:, run, :].rearrange("p m j -> p (m j)"))
 
-        def interleave_w(n, c, engine, tag):
-            w_grouped[n, c] = work.tile([P, UNIT_PART], BF16, name=tag, bufs=SLOTS[tag], align_bytes=64)
+        def place_of_pass(n, c):
+            return c if n % 2 else 1 - c
+
+        def w_grouped(n):
+            if n < W_AHEAD:
+                return w_first[n][:]
+            return w_shared[:, n % 2 * UNIT_PART:(n % 2 + PASSES) * UNIT_PART]
+
+        def interleave_w(n, c, engine):
             g, v = divmod(n, 2)
-            dst = w_grouped[n, c][:].rearrange("p (e m j) -> p m j e", e=2, j=PACK)
+            first = place_of_pass(n, c) * UNIT_PART
+            dst = w_grouped(n)[:, first:first + UNIT_PART].rearrange("p (e m j) -> p m j e", e=2, j=PACK)
             src = w_raw[g * PASSES + c].rearrange("p j (m v e) -> p v m j e", v=2, e=2)[:, v]
             if engine == "gpsimd":
                 nc.gpsimd.tensor_scalar(out=dst.rearrange("p m j e -> p m e j"), in0=src.rearrange("p m j e -> p m e j"),
@@ -142,13 +151,14 @@ def tile_squared_relu_up_projection_b1_kernel(tc, X_bytes, X_scale, W, b, out_0,
             else:
                 nc.vector.tensor_copy(out=dst, in_=src)
 
-        def quantize_w(n, c):
+        def quantize_w(n, c=None):
             if n not in w_codes:
                 w_codes[n] = work.tile([P, GROUP], U32, name="w_codes", bufs=W_CODE_SLOTS, align_bytes=64)
                 w_scales[n] = work.tile([P, GROUP], U8, name="w_scales", bufs=W_CODE_SLOTS, align_bytes=64)
-            cols = slice(c * 2 * P, (c + 1) * 2 * P)
-            nc.vector.quantize_mx(out=w_codes[n][:, cols].bitcast(FP8X4), scales=w_scales[n][:, cols],
-                                  in_=w_grouped[n, c][:])
+            first, end = (0, PASSES) if c is None else (place_of_pass(n, c), place_of_pass(n, c) + 1)
+            words = slice(first * 2 * P, end * 2 * P)
+            nc.vector.quantize_mx(out=w_codes[n][:, words].bitcast(FP8X4), scales=w_scales[n][:, words],
+                                  in_=w_grouped(n)[:, first * UNIT_PART:end * UNIT_PART])
 
         def warm_up_tensor_engine(operand, columns, count):
             bank = psum.tile([P, GROUP], F32, name="h")
@@ -162,7 +172,8 @@ def tile_squared_relu_up_projection_b1_kernel(tc, X_bytes, X_scale, W, b, out_0,
             n = 2 * g + t // 2
             for run in RUNS:
                 for c in range(PASSES):
-                    cols = slice((2 * c + t % 2) * P, (2 * c + t % 2 + 1) * P)
+                    first = (2 * place_of_pass(n, c) + t % 2) * P
+                    cols = slice(first, first + P)
                     nc.tensor.matmul_mx(out=bank[:, run],
                                         lhsT=w_codes[n][:, cols].bitcast(FP8X4), lhsT_scale=w_scales[n][:, cols],
                                         rhs=x_codes[h][:, c, run].bitcast(FP8X4), rhs_scale=x_scales[h][:, c, run],
@@ -187,7 +198,8 @@ def tile_squared_relu_up_projection_b1_kernel(tc, X_bytes, X_scale, W, b, out_0,
                 nc.tensor.transpose(bank[:, t * P:(t + 1) * P], clamped[step][:, t, i * P:(i + 1) * P], ident[:])
 
         def plane_views(tile, step, first, end):
-            dst = tile[:, first * PACK:end * PACK].rearrange("p (a i t) -> p a t i", i=2, t=PACK)
+            offset = step % 2 * HALF
+            dst = tile[:, (offset + first) * PACK:(offset + end) * PACK].rearrange("p (a i t) -> p a t i", i=2, t=PACK)
             src = clamped[step][:, :, first:end].rearrange("p t (a i) -> p a t i", i=2)
             return dst, src
 
@@ -197,9 +209,10 @@ def tile_squared_relu_up_projection_b1_kernel(tc, X_bytes, X_scale, W, b, out_0,
             return VECTOR_TOKENS[step - STEPS]
 
         def square_for_planes(step, engine, first, end):
-            if step not in y_bf16:
-                y_bf16[step] = work.tile([P, PACK * HALF], BF16, name="staging", bufs=SLOTS["staging"], align_bytes=64)
-            dst, src = plane_views(y_bf16[step], step, first, end)
+            g = step // 2
+            if g not in y_bf16:
+                y_bf16[g] = work.tile([P, PACK * T], BF16, name="y_bf16", bufs=2, align_bytes=64)
+            dst, src = plane_views(y_bf16[g], step, first, end)
             if engine == "scalar":
                 nc.scalar.activation(out=dst, in_=src, func=ACT.Square)
             else:
@@ -223,15 +236,12 @@ def tile_squared_relu_up_projection_b1_kernel(tc, X_bytes, X_scale, W, b, out_0,
                 dst = out_2[a * PACKED:(a + 1) * PACKED, 4 * q:4 * q + 4, :]
                 nc.sync.dma_start(out=dst.bitcast(I32), in_=y_scales[a][32 * q:32 * q + 4 * PACKED, :].bitcast(I32))
 
-        def quantize_y(step, runs):
-            g, h = divmod(step, 2)
+        def quantize_y(g, first, end):
             if g not in y_codes:
                 y_codes[g] = work.tile([P, T], U32, name="y_codes", bufs=RESULT_SLOTS // 2, align_bytes=64)
             plane = y_scales[g // PACKED][4 * (g % PACKED):, :]
-            for run in runs:
-                tokens = slice(h * HALF + run.start, h * HALF + run.stop)
-                nc.vector.quantize_mx(out=y_codes[g][:, tokens].bitcast(FP8X4), scales=plane[:, tokens],
-                                      in_=y_bf16[step][:, run.start * PACK:run.stop * PACK])
+            nc.vector.quantize_mx(out=y_codes[g][:, first:end].bitcast(FP8X4), scales=plane[:, first:end],
+                                  in_=y_bf16[g][:, first * PACK:end * PACK])
 
         def store_planes(step):
             g, h = divmod(step, 2)
@@ -245,22 +255,21 @@ def tile_squared_relu_up_projection_b1_kernel(tc, X_bytes, X_scale, W, b, out_0,
         widen_x(0, on_vector=True)
         widen_x(1, on_vector=False)
         widen_x(2, on_vector=True)
-        interleave_w(0, 0, "vector", "w_first")
-        interleave_w(1, 0, "vector", "w_first")
+        interleave_w(0, 0, "vector")
+        interleave_w(1, 0, "vector")
         turn_x(0)
         turn_x(2)
         turn_x(1)
-        warm_up_tensor_engine(w_grouped[0, 0], GROUP, 4)
-        interleave_w(0, 1, "vector", "w_first")
-        interleave_w(1, 1, "scalar", "w_first")
+        warm_up_tensor_engine(w_first[1], GROUP, 4)
+        interleave_w(0, 1, "vector")
+        interleave_w(1, 1, "scalar")
         quantize_w(0, 0)
         quantize_x(0)
         quantize_w(0, 1)
         widen_x(3, on_vector=False)
         widen_x(4, on_vector=True)
         widen_x(5, on_vector=True)
-        quantize_w(1, 0)
-        quantize_w(1, 1)
+        quantize_w(1)
         multiply(0, 0)
         multiply(0, 1)
         add_bias_and_clamp(0, (0,), on_vector=False)
@@ -270,12 +279,11 @@ def tile_squared_relu_up_projection_b1_kernel(tc, X_bytes, X_scale, W, b, out_0,
         multiply(0, 2)
         multiply(0, 3)
         add_bias_and_clamp(0, (1, 2, 3), on_vector=False)
-        interleave_w(2, 0, "vector", "staging")
-        interleave_w(2, 1, "vector", "staging")
+        interleave_w(2, 0, "vector")
+        interleave_w(2, 1, "vector")
         quantize_x(1)
-        quantize_w(2, 1)
-        quantize_w(2, 0)
-        interleave_w(3, 1, "vector", "w_vector")
+        quantize_w(2)
+        interleave_w(3, 1, "vector")
 
         for step in range(STEPS):
             n = step + W_AHEAD
@@ -283,17 +291,20 @@ def tile_squared_relu_up_projection_b1_kernel(tc, X_bytes, X_scale, W, b, out_0,
             if last:
                 for i in range(TILES):
                     add_bias_and_clamp(step, range(PACK), on_vector=True, tokens=slice(i * P, (i + 1) * P))
-                quantize_y(step - 1, RUNS[:1])
+                quantize_y(GROUPS - 1, 0, RUNS[0].stop)
             elif step > 0:
                 add_bias_and_clamp(step, range(PACK), on_vector=True)
                 if n < UNITS:
-                    interleave_w(n, 0, "gpsimd", "staging")
-                    quantize_w(n, 1)
-                    quantize_w(n, 0)
-                quantize_y(step - 1, RUNS)
+                    interleave_w(n, 0, "gpsimd")
+                if step % 2:
+                    quantize_y(step // 2, 0, RUNS[0].stop)
+                else:
+                    quantize_y(step // 2 - 1, RUNS[0].stop, T)
                 store_planes(step - 1)
+                if n < UNITS:
+                    quantize_w(n)
                 if n + 1 < UNITS:
-                    interleave_w(n + 1, 1, "vector", "w_vector")
+                    interleave_w(n + 1, 1, "vector")
             tiles_between = TILES - 1 if step else 0
             for t in range(PACK // 2):
                 if not last:
@@ -311,8 +322,9 @@ def tile_squared_relu_up_projection_b1_kernel(tc, X_bytes, X_scale, W, b, out_0,
                 square_for_planes(step, "vector", cut, HALF)
             for i in range(TILES - 1 if last else TILES):
                 square_and_store(step, i, nc.sync)
-        quantize_y(STEPS - 2, RUNS[1:])
+        quantize_y(GROUPS - 1, RUNS[0].stop, HALF)
         store_planes(STEPS - 2)
-        quantize_y(STEPS - 1, RUNS)
+        for run in RUNS:
+            quantize_y(GROUPS - 1, HALF + run.start, HALF + run.stop)
         store_planes(STEPS - 1)
         square_and_store(STEPS - 1, TILES - 1, nc.scalar)

@@ -31,7 +31,8 @@ X_BLOCK = 128
 QUADRANTS = 4
 
 W_AHEAD = 2
-VECTOR_TOKENS = (128, 192, 256)
+VECTOR_TOKENS = (128, 192, 256, 192)
+FIRST_LATE_STEP = 12
 PACKED = 4
 W_CODE_SLOTS = 6
 RESULT_SLOTS = 6
@@ -204,8 +205,6 @@ def tile_squared_relu_up_projection_b1_kernel(tc, X_bytes, X_scale, W, b, out_0,
             return dst, src
 
         def vector_tokens(step):
-            if step + 1 + W_AHEAD < UNITS:
-                return 0
             return VECTOR_TOKENS[step - STEPS]
 
         def square_for_planes(step, engine, first, end):
@@ -234,7 +233,8 @@ def tile_squared_relu_up_projection_b1_kernel(tc, X_bytes, X_scale, W, b, out_0,
         def store_scales(a):
             for q in range(QUADRANTS):
                 dst = out_2[a * PACKED:(a + 1) * PACKED, 4 * q:4 * q + 4, :]
-                nc.sync.dma_start(out=dst.bitcast(I32), in_=y_scales[a][32 * q:32 * q + 4 * PACKED, :].bitcast(I32))
+                queue = nc.scalar if q % 2 and (a + 1) * PACKED == GROUPS else nc.sync
+                queue.dma_start(out=dst.bitcast(I32), in_=y_scales[a][32 * q:32 * q + 4 * PACKED, :].bitcast(I32))
 
         def quantize_y(g, first, end):
             if g not in y_codes:
@@ -242,6 +242,17 @@ def tile_squared_relu_up_projection_b1_kernel(tc, X_bytes, X_scale, W, b, out_0,
             plane = y_scales[g // PACKED][4 * (g % PACKED):, :]
             nc.vector.quantize_mx(out=y_codes[g][:, first:end].bitcast(FP8X4), scales=plane[:, first:end],
                                   in_=y_bf16[g][:, first * PACK:end * PACK])
+
+        def quantize_planes(step):
+            g, h = divmod(step, 2)
+            if g == GROUPS - 1:
+                for run in RUNS:
+                    quantize_y(g, h * HALF + run.start, h * HALF + run.stop)
+            elif h == 0:
+                quantize_y(g, 0, RUNS[0].stop)
+            else:
+                quantize_y(g, RUNS[0].stop, T)
+            store_planes(step)
 
         def store_planes(step):
             g, h = divmod(step, 2)
@@ -288,23 +299,24 @@ def tile_squared_relu_up_projection_b1_kernel(tc, X_bytes, X_scale, W, b, out_0,
         for step in range(STEPS):
             n = step + W_AHEAD
             last = step == STEPS - 1
+            late = step >= FIRST_LATE_STEP
             if last:
                 for i in range(TILES):
                     add_bias_and_clamp(step, range(PACK), on_vector=True, tokens=slice(i * P, (i + 1) * P))
-                quantize_y(GROUPS - 1, 0, RUNS[0].stop)
             elif step > 0:
                 add_bias_and_clamp(step, range(PACK), on_vector=True)
-                if n < UNITS:
-                    interleave_w(n, 0, "gpsimd")
-                if step % 2:
-                    quantize_y(step // 2, 0, RUNS[0].stop)
-                else:
-                    quantize_y(step // 2 - 1, RUNS[0].stop, T)
-                store_planes(step - 1)
-                if n < UNITS:
-                    quantize_w(n)
-                if n + 1 < UNITS:
-                    interleave_w(n + 1, 1, "vector")
+            if 0 < step and n < UNITS:
+                interleave_w(n, 0, "gpsimd")
+            if 0 < step <= FIRST_LATE_STEP:
+                quantize_planes(step - 1)
+            if 0 < step and n < UNITS:
+                quantize_w(n)
+            if 0 < step and n + 1 < UNITS:
+                interleave_w(n + 1, 1, "vector")
+            if step > FIRST_LATE_STEP:
+                square_for_planes(step - 1, "vector", HALF - vector_tokens(step - 1), HALF)
+            if FIRST_LATE_STEP + 1 < step < STEPS - 1:
+                quantize_planes(step - 2)
             tiles_between = TILES - 1 if step else 0
             for t in range(PACK // 2):
                 if not last:
@@ -316,15 +328,17 @@ def tile_squared_relu_up_projection_b1_kernel(tc, X_bytes, X_scale, W, b, out_0,
                     multiply(step + 1, t)
             for i in range(tiles_between, TILES):
                 turn_clamped(step, i)
-            cut = HALF - vector_tokens(step)
-            square_for_planes(step, "scalar", 0, cut)
-            if cut < HALF:
-                square_for_planes(step, "vector", cut, HALF)
-            for i in range(TILES - 1 if last else TILES):
+            if not late:
+                square_for_planes(step, "scalar", 0, HALF)
+            tiles_first = TILES if last else TILES - 1
+            for i in range(TILES):
+                if late and i == tiles_first:
+                    square_for_planes(step, "scalar", 0, HALF - vector_tokens(step))
+                    if step == STEPS - 2:
+                        quantize_planes(step - 1)
                 square_and_store(step, i, nc.sync)
-        quantize_y(GROUPS - 1, RUNS[0].stop, HALF)
-        store_planes(STEPS - 2)
-        for run in RUNS:
-            quantize_y(GROUPS - 1, HALF + run.start, HALF + run.stop)
-        store_planes(STEPS - 1)
-        square_and_store(STEPS - 1, TILES - 1, nc.scalar)
+            if late and tiles_first == TILES:
+                square_for_planes(step, "scalar", 0, HALF - vector_tokens(step))
+        square_for_planes(STEPS - 1, "vector", HALF - vector_tokens(STEPS - 1), HALF)
+        quantize_planes(STEPS - 2)
+        quantize_planes(STEPS - 1)

@@ -200,8 +200,8 @@ def tile_squared_relu_up_projection_b1_kernel(tc, X_bytes, X_scale, W, b, out_0,
 
         def plane_views(tile, step, first, end):
             offset = step % 2 * HALF
-            dst = tile[:, (offset + first) * PACK:(offset + end) * PACK].rearrange("p (a i t) -> p a t i", i=2, t=PACK)
-            src = clamped[step][:, :, first:end].rearrange("p t (a i) -> p a t i", i=2)
+            dst = tile[:, (offset + first) * PACK:(offset + end) * PACK].rearrange("p (a i t) -> p a t i", i=4, t=PACK)
+            src = clamped[step][:, :, first:end].rearrange("p t (a i) -> p a t i", i=4)
             return dst, src
 
         def vector_tokens(step):

@@ -31,6 +31,7 @@ X_BLOCK = 128
 QUADRANTS = 4
 
 W_AHEAD = 2
+HEAD_SHARE = 40
 VECTOR_TOKENS = (128, 192, 256, 192)
 FIRST_LATE_STEP = 12
 PACKED = 4
@@ -83,9 +84,10 @@ def tile_squared_relu_up_projection_b1_kernel(tc, X_bytes, X_scale, W, b, out_0,
         nc.scalar.activation(out=table_warm_up[:], in_=ident[:, 0:1], func=ACT.Square)
         for i in range(TILES):
             load_x(i)
-        load_w(0, 1)
         load_x_scale(1, nc.sync)
-        for i in range(TILES, 2 * TILES):
+        load_x(TILES)
+        load_w(0, 1)
+        for i in range(TILES + 1, 2 * TILES):
             load_x(i)
         nc.sync.dma_start(out=bias[:], in_=b.rearrange("o (g p t) -> p (o g) t", p=P, t=PACK))
         for first_group, end_group in W_LOADS:
@@ -139,11 +141,12 @@ def tile_squared_relu_up_projection_b1_kernel(tc, X_bytes, X_scale, W, b, out_0,
                 return w_first[n][:]
             return w_shared[:, n % 2 * UNIT_PART:(n % 2 + PASSES) * UNIT_PART]
 
-        def interleave_w(n, c, engine):
+        def interleave_w(n, c, engine, m_range=slice(0, P)):
             g, v = divmod(n, 2)
             first = place_of_pass(n, c) * UNIT_PART
             dst = w_grouped(n)[:, first:first + UNIT_PART].rearrange("p (e m j) -> p m j e", e=2, j=PACK)
             src = w_raw[g * PASSES + c].rearrange("p j (m v e) -> p v m j e", v=2, e=2)[:, v]
+            dst, src = dst[:, m_range], src[:, m_range]
             if engine == "gpsimd":
                 nc.gpsimd.tensor_scalar(out=dst.rearrange("p m j e -> p m e j"), in0=src.rearrange("p m j e -> p m e j"),
                                         scalar1=1.0, scalar2=0.0, op0=ALU.mult, op1=ALU.add)
@@ -266,30 +269,31 @@ def tile_squared_relu_up_projection_b1_kernel(tc, X_bytes, X_scale, W, b, out_0,
         widen_x(0, on_vector=True)
         widen_x(1, on_vector=False)
         widen_x(2, on_vector=True)
+        widen_x(3, on_vector=True)
         interleave_w(0, 0, "vector")
-        interleave_w(1, 0, "vector")
+        interleave_w(1, 0, "vector", slice(HEAD_SHARE, P))
         turn_x(0)
         turn_x(2)
+        interleave_w(1, 0, "scalar", slice(0, HEAD_SHARE))
         turn_x(1)
-        warm_up_tensor_engine(w_first[1], GROUP, 4)
         interleave_w(0, 1, "vector")
         interleave_w(1, 1, "scalar")
+        widen_x(4, on_vector=True)
+        widen_x(5, on_vector=False)
+        warm_up_tensor_engine(w_first[0][:, UNIT_PART:], GROUP, 3)
+        turn_x(3)
+        turn_x(4)
+        warm_up_tensor_engine(w_first[0][:, UNIT_PART:], GROUP, 2)
         quantize_w(0, 0)
         quantize_x(0)
         quantize_w(0, 1)
-        widen_x(3, on_vector=False)
-        widen_x(4, on_vector=True)
-        widen_x(5, on_vector=True)
         quantize_w(1)
+        turn_x(5)
         multiply(0, 0)
         multiply(0, 1)
-        add_bias_and_clamp(0, (0,), on_vector=False)
-        turn_x(4)
-        turn_x(3)
-        turn_x(5)
         multiply(0, 2)
         multiply(0, 3)
-        add_bias_and_clamp(0, (1, 2, 3), on_vector=False)
+        add_bias_and_clamp(0, range(PACK), on_vector=False)
         interleave_w(2, 0, "vector")
         interleave_w(2, 1, "vector")
         quantize_x(1)
@@ -317,7 +321,7 @@ def tile_squared_relu_up_projection_b1_kernel(tc, X_bytes, X_scale, W, b, out_0,
                 square_for_planes(step - 1, "vector", HALF - vector_tokens(step - 1), HALF)
             if FIRST_LATE_STEP + 1 < step < STEPS - 1:
                 quantize_planes(step - 2)
-            tiles_between = TILES - 1 if step else 0
+            tiles_between = min(step, TILES - 1)
             for t in range(PACK // 2):
                 if not last:
                     multiply(step + 1, t)

@@ -32,7 +32,7 @@ QUADRANTS = 4
 
 W_AHEAD = 2
 HEAD_SHARE = 40
-VECTOR_TOKENS = (128, 192, 256, 192)
+VECTOR_TOKENS = (128, 128, 256, 192)
 FIRST_LATE_STEP = 12
 PACKED = 4
 W_CODE_SLOTS = 6
@@ -259,8 +259,12 @@ def tile_squared_relu_up_projection_b1_kernel(tc, X_bytes, X_scale, W, b, out_0,
 
         def store_planes(step):
             g, h = divmod(step, 2)
-            if g == GROUPS - 1 or h == 1:
-                tokens = slice(h * HALF, (h + 1) * HALF) if g == GROUPS - 1 else slice(0, T)
+            if g >= GROUPS - 2 or h == 1:
+                tokens = slice(0, T)
+                if g == GROUPS - 1:
+                    tokens = slice(h * HALF, (h + 1) * HALF)
+                elif g == GROUPS - 2:
+                    tokens = slice(RUNS[0].stop, T) if h else RUNS[0]
                 dst = out_1[g, :, tokens, :].rearrange("p m t -> p (m t)")
                 nc.sync.dma_start(out=dst.bitcast(I32), in_=y_codes[g][:, tokens].bitcast(I32))
             if h == 1 and g % PACKED == PACKED - 1:
@@ -321,7 +325,7 @@ def tile_squared_relu_up_projection_b1_kernel(tc, X_bytes, X_scale, W, b, out_0,
                 square_for_planes(step - 1, "vector", HALF - vector_tokens(step - 1), HALF)
             if FIRST_LATE_STEP + 1 < step < STEPS - 1:
                 quantize_planes(step - 2)
-            tiles_between = min(step, TILES - 1)
+            tiles_between = TILES if step == UNITS - 1 - W_AHEAD else min(step, TILES - 1)
             for t in range(PACK // 2):
                 if not last:
                     multiply(step + 1, t)
@@ -334,7 +338,7 @@ def tile_squared_relu_up_projection_b1_kernel(tc, X_bytes, X_scale, W, b, out_0,
                 turn_clamped(step, i)
             if not late:
                 square_for_planes(step, "scalar", 0, HALF)
-            tiles_first = TILES if last else TILES - 1
+            tiles_first = TILES if step % 2 else TILES - 1
             for i in range(TILES):
                 if late and i == tiles_first:
                     square_for_planes(step, "scalar", 0, HALF - vector_tokens(step))

@@ -32,7 +32,7 @@ QUADRANTS = 4
 
 W_AHEAD = 2
 HEAD_SHARE = 40
-VECTOR_TOKENS = (128, 128, 256, 192)
+VECTOR_TOKENS = (128, 128, 192, 256)
 FIRST_LATE_STEP = 12
 PACKED = 4
 W_CODE_SLOTS = 6
@@ -89,9 +89,10 @@ def tile_squared_relu_up_projection_b1_kernel(tc, X_bytes, X_scale, W, b, out_0,
         load_w(0, 1)
         for i in range(TILES + 1, 2 * TILES):
             load_x(i)
-        nc.sync.dma_start(out=bias[:], in_=b.rearrange("o (g p t) -> p (o g) t", p=P, t=PACK))
         for first_group, end_group in W_LOADS:
             load_w(first_group, end_group)
+            if first_group == 1:
+                nc.sync.dma_start(out=bias[:], in_=b.rearrange("o (g p t) -> p (o g) t", p=P, t=PACK))
 
         x_words, w_codes, w_scales = {}, {}, {}
         h_banks, clamped, turned, y_bf16, y_codes, y_rows = {}, {}, {}, {}, {}, {}
@@ -309,8 +310,8 @@ def tile_squared_relu_up_projection_b1_kernel(tc, X_bytes, X_scale, W, b, out_0,
             last = step == STEPS - 1
             late = step >= FIRST_LATE_STEP
             if last:
-                for i in range(TILES):
-                    add_bias_and_clamp(step, range(PACK), on_vector=True, tokens=slice(i * P, (i + 1) * P))
+                for tokens in RUNS:
+                    add_bias_and_clamp(step, range(PACK), on_vector=True, tokens=tokens)
             elif step > 0:
                 add_bias_and_clamp(step, range(PACK), on_vector=True)
             if 0 < step and n < UNITS:

@@ -32,11 +32,15 @@ QUADRANTS = 4
 
 W_AHEAD = 2
 HEAD_SHARE = 40
-VECTOR_TOKENS = (128, 128, 192, 256)
-FIRST_LATE_STEP = 12
+FIRST_LATE_STEP = UNITS - W_AHEAD - 2
+VECTOR_TOKENS = (128, 64, 128, 256)
+GPSIMD_STEPS = (STEPS - 3, STEPS - 2)
+WARM_UPS = (3, 2)
 PACKED = 4
 W_CODE_SLOTS = 6
 RESULT_SLOTS = 6
+CLAMPED_SLOTS = 3
+PLANE_SLOTS = 2
 W_LOADS = ((1, 2), (2, 4), (4, 8))
 LAST_WHOLE_STORE = STEPS // 2 - 1
 
@@ -45,14 +49,14 @@ def tile_squared_relu_up_projection_b1_kernel(tc, X_bytes, X_scale, W, b, out_0,
     nc = tc.nc
     with ExitStack() as ctx:
         keep = ctx.enter_context(tc.tile_pool(name="keep", bufs=1))
-        work = ctx.enter_context(tc.tile_pool(name="work", bufs=3))
+        work = ctx.enter_context(tc.tile_pool(name="work", bufs=CLAMPED_SLOTS))
         psum = ctx.enter_context(tc.psum_pool(name="psum", bufs=4))
         ctx.enter_context(tc.manual_schedule())
 
         ident = keep.tile([P, P], F32, name="ident")
         make_identity(nc, ident[:])
 
-        x_scale = [keep.tile([P, TILES, K // X_BLOCK], F32, name="x_scale%d" % h) for h in range(2)]
+        x_factor = [keep.tile([P, TILES, K // X_BLOCK], F32, name="x_factor%d" % h) for h in range(2)]
         bias = keep.tile([P, GROUPS, PACK], BF16, name="bias")
         x_raw = [keep.tile([P, K], U8, name="x_raw%d" % i) for i in range(2 * TILES)]
         w_raw = {}
@@ -61,11 +65,12 @@ def tile_squared_relu_up_projection_b1_kernel(tc, X_bytes, X_scale, W, b, out_0,
         x_scales = [keep.tile([P, PASSES, HALF], U8, name="x_scales%d" % h, align_bytes=64) for h in range(2)]
         w_first = [keep.tile([P, PASSES * UNIT_PART], BF16, name="w_first%d" % n, align_bytes=64) for n in range(W_AHEAD)]
         w_shared = keep.tile([P, 3 * UNIT_PART], BF16, name="w_shared", align_bytes=64)
+        y_gpsimd = w_shared[:, UNIT_PART:UNIT_PART + P * PACK]
         y_scales = [keep.tile([P, T], U8, name="y_scales%d" % a, align_bytes=64) for a in range(GROUPS // PACKED)]
 
-        def load_x_scale(h, queue):
+        def load_x_factor(h, queue):
             rows = X_scale[h * HALF:(h + 1) * HALF, :]
-            queue.dma_start(out=x_scale[h][:], in_=rows.rearrange("(i p) j -> p i j", p=P))
+            queue.dma_start(out=x_factor[h][:], in_=rows.rearrange("(i p) j -> p i j", p=P))
 
         def load_x(i):
             nc.sync.dma_start(out=x_raw[i][:], in_=X_bytes[i * P:(i + 1) * P, :])
@@ -77,14 +82,14 @@ def tile_squared_relu_up_projection_b1_kernel(tc, X_bytes, X_scale, W, b, out_0,
                 rows = W[c * GROUP:(c + 1) * GROUP, first_group * GROUP:end_group * GROUP]
                 nc.sync.dma_start(out=tile[:], in_=rows.rearrange("(p j) n -> p j n", j=PACK))
                 for g in range(first_group, end_group):
-                    w_raw[g * PASSES + c] = tile[:, :, (g - first_group) * GROUP:(g - first_group + 1) * GROUP]
+                    w_raw[g, c] = tile[:, :, (g - first_group) * GROUP:(g - first_group + 1) * GROUP]
 
-        load_x_scale(0, nc.scalar)
+        load_x_factor(0, nc.scalar)
         table_warm_up = keep.tile([P, 1], F32, name="table_warm_up")
         nc.scalar.activation(out=table_warm_up[:], in_=ident[:, 0:1], func=ACT.Square)
         for i in range(TILES):
             load_x(i)
-        load_x_scale(1, nc.sync)
+        load_x_factor(1, nc.sync)
         load_x(TILES)
         load_w(0, 1)
         for i in range(TILES + 1, 2 * TILES):
@@ -95,22 +100,22 @@ def tile_squared_relu_up_projection_b1_kernel(tc, X_bytes, X_scale, W, b, out_0,
                 nc.sync.dma_start(out=bias[:], in_=b.rearrange("o (g p t) -> p (o g) t", p=P, t=PACK))
 
         x_words, w_codes, w_scales = {}, {}, {}
-        h_banks, clamped, turned, y_bf16, y_codes, y_rows = {}, {}, {}, {}, {}, {}
+        sum_banks, clamped, turned, y_bf16, y_codes, y_rows = {}, {}, {}, {}, {}, {}
 
         def widen_x(i, on_vector):
             for c in range(PASSES):
                 wide = work.tile([P, GROUP], BF16, name="x_wide", bufs=PASSES * 2 * TILES)
-                for q in range(GROUP // X_BLOCK):
-                    j = c * (GROUP // X_BLOCK) + q
-                    src = x_raw[i][:, j * X_BLOCK:(j + 1) * X_BLOCK].bitcast(FP8)
-                    scale = x_scale[i // TILES][:, i % TILES, j:j + 1]
+                for r in range(GROUP // X_BLOCK):
+                    block = c * (GROUP // X_BLOCK) + r
+                    src = x_raw[i][:, block * X_BLOCK:(block + 1) * X_BLOCK].bitcast(FP8)
+                    factor = x_factor[i // TILES][:, i % TILES, block:block + 1]
                     if on_vector:
-                        dst = wide[:].rearrange("p (u q a e) -> p q a u e", u=2, q=GROUP // X_BLOCK, e=2)[:, q]
+                        dst = wide[:].rearrange("p (u r a e) -> p r a u e", u=2, r=GROUP // X_BLOCK, e=2)[:, r]
                         nc.vector.tensor_scalar(out=dst, in0=src.rearrange("p (a u e) -> p a u e", u=2, e=2),
-                                                scalar1=scale, scalar2=None, op0=ALU.mult)
+                                                scalar1=factor, scalar2=None, op0=ALU.mult)
                     else:
-                        nc.scalar.activation(out=wide[:, q * X_BLOCK:(q + 1) * X_BLOCK], in_=src,
-                                             func=ACT.Copy, scale=scale)
+                        nc.scalar.activation(out=wide[:, r * X_BLOCK:(r + 1) * X_BLOCK], in_=src,
+                                             func=ACT.Copy, scale=factor)
                 words = wide[:].bitcast(F32)
                 for u in range(2):
                     x_words[i, c, u] = words[:, u * P:(u + 1) * P] if on_vector else words[:, u:2 * P:2]
@@ -146,7 +151,7 @@ def tile_squared_relu_up_projection_b1_kernel(tc, X_bytes, X_scale, W, b, out_0,
             g, v = divmod(n, 2)
             first = place_of_pass(n, c) * UNIT_PART
             dst = w_grouped(n)[:, first:first + UNIT_PART].rearrange("p (e m j) -> p m j e", e=2, j=PACK)
-            src = w_raw[g * PASSES + c].rearrange("p j (m v e) -> p v m j e", v=2, e=2)[:, v]
+            src = w_raw[g, c].rearrange("p j (m v e) -> p v m j e", v=2, e=2)[:, v]
             dst, src = dst[:, m_range], src[:, m_range]
             if engine == "gpsimd":
                 nc.gpsimd.tensor_scalar(out=dst.rearrange("p m j e -> p m e j"), in0=src.rearrange("p m j e -> p m e j"),
@@ -165,15 +170,16 @@ def tile_squared_relu_up_projection_b1_kernel(tc, X_bytes, X_scale, W, b, out_0,
             nc.vector.quantize_mx(out=w_codes[n][:, words].bitcast(FP8X4), scales=w_scales[n][:, words],
                                   in_=w_grouped(n)[:, first * UNIT_PART:end * UNIT_PART])
 
-        def warm_up_tensor_engine(operand, columns, count):
-            bank = psum.tile([P, GROUP], F32, name="h")
+        def warm_up_tensor_engine(count):
+            operand = w_first[0][:, UNIT_PART:]
+            bank = psum.tile([P, GROUP], F32, name="sums")
             for r in range(count):
-                nc.tensor.matmul(bank[:, :columns], lhsT=operand[:, :P], rhs=operand[:, :columns], start=True, stop=True)
+                nc.tensor.matmul(bank[:], lhsT=operand[:, :P], rhs=operand[:, :GROUP], start=True, stop=True)
 
         def multiply(step, t):
             g, h = divmod(step, 2)
-            bank = psum.tile([P, GROUP], F32, name="h")
-            h_banks[step, t] = bank
+            bank = psum.tile([P, GROUP], F32, name="sums")
+            sum_banks[step, t] = bank
             n = 2 * g + t // 2
             for run in RUNS:
                 for c in range(PASSES):
@@ -184,12 +190,12 @@ def tile_squared_relu_up_projection_b1_kernel(tc, X_bytes, X_scale, W, b, out_0,
                                         rhs=x_codes[h][:, c, run].bitcast(FP8X4), rhs_scale=x_scales[h][:, c, run],
                                         start=(c == 0), stop=(c == PASSES - 1))
 
-        def add_bias_and_clamp(step, slices, on_vector, tokens=slice(0, HALF)):
+        def add_bias_and_clamp(step, on_vector, tokens=slice(0, HALF)):
             g = step // 2
             if step not in clamped:
                 clamped[step] = work.tile([P, PACK, HALF], F32, name="clamped")
-            for t in slices:
-                src, dst = h_banks[step, t][:, tokens], clamped[step][:, t, tokens]
+            for t in range(PACK):
+                src, dst = sum_banks[step, t][:, tokens], clamped[step][:, t, tokens]
                 if on_vector:
                     nc.vector.tensor_scalar(out=dst, in0=src, scalar1=bias[:, g, t:t + 1], scalar2=0.0,
                                             op0=ALU.add, op1=ALU.max)
@@ -202,26 +208,29 @@ def tile_squared_relu_up_projection_b1_kernel(tc, X_bytes, X_scale, W, b, out_0,
             for t in range(PACK):
                 nc.tensor.transpose(bank[:, t * P:(t + 1) * P], clamped[step][:, t, i * P:(i + 1) * P], ident[:])
 
-        def plane_views(tile, step, first, end):
-            offset = step % 2 * HALF
-            dst = tile[:, (offset + first) * PACK:(offset + end) * PACK].rearrange("p (a i t) -> p a t i", i=4, t=PACK)
-            src = clamped[step][:, :, first:end].rearrange("p t (a i) -> p a t i", i=4)
-            return dst, src
+        def plane_shares(step):
+            end = RUNS[0].stop if step in GPSIMD_STEPS else HALF
+            return end - (VECTOR_TOKENS[step - FIRST_LATE_STEP] if step >= FIRST_LATE_STEP else 0), end
 
-        def vector_tokens(step):
-            return VECTOR_TOKENS[step - STEPS]
-
-        def square_for_planes(step, engine, first, end):
-            g = step // 2
+        def square_for_planes(step, on_vector):
+            g, h = divmod(step, 2)
             if g not in y_bf16:
-                y_bf16[g] = work.tile([P, PACK * T], BF16, name="y_bf16", bufs=2, align_bytes=64)
-            dst, src = plane_views(y_bf16[g], step, first, end)
-            if engine == "scalar":
-                nc.scalar.activation(out=dst, in_=src, func=ACT.Square)
-            else:
+                y_bf16[g] = work.tile([P, PACK * T], BF16, name="y_bf16", bufs=PLANE_SLOTS, align_bytes=64)
+            first, end = plane_shares(step) if on_vector else (0, plane_shares(step)[0])
+            dst = y_bf16[g][:, (h * HALF + first) * PACK:(h * HALF + end) * PACK]
+            dst = dst.rearrange("p (a i t) -> p a t i", i=4, t=PACK)
+            src = clamped[step][:, :, first:end].rearrange("p t (a i) -> p a t i", i=4)
+            if on_vector:
                 nc.vector.tensor_tensor(out=dst, in0=src, in1=src, op=ALU.mult)
+            else:
+                nc.scalar.activation(out=dst, in_=src, func=ACT.Square)
 
-        def square_and_store(step, i, queue):
+        def square_on_gpsimd(step):
+            dst = y_gpsimd.rearrange("p (a i t) -> p a t i", i=4, t=PACK)
+            src = clamped[step][:, :, RUNS[1]].rearrange("p t (a i) -> p a t i", i=4)
+            nc.gpsimd.tensor_tensor(out=dst, in0=src, in1=src, op=ALU.mult)
+
+        def square_and_store(step, i):
             g, h = divmod(step, 2)
             if i == 0:
                 y_rows[step] = work.tile([P, TILES, GROUP], F32, name="y", bufs=RESULT_SLOTS)
@@ -230,9 +239,13 @@ def tile_squared_relu_up_projection_b1_kernel(tc, X_bytes, X_scale, W, b, out_0,
                                  in_=turned[step, i][:].rearrange("p (t m) -> p m t", t=PACK), func=ACT.Square)
             dst = out_0[h * HALF:(h + 1) * HALF, g * GROUP:(g + 1) * GROUP].rearrange("(i p) f -> p i f", p=P)
             if step > LAST_WHOLE_STORE:
-                queue.dma_start(out=dst[:, i, :], in_=y[:, i, :])
+                nc.sync.dma_start(out=dst[:, i, :], in_=y[:, i, :])
             elif i == TILES - 1:
-                queue.dma_start(out=dst, in_=y[:])
+                nc.sync.dma_start(out=dst, in_=y[:])
+
+        def store_codes(g, tokens):
+            dst = out_1[g, :, tokens, :].rearrange("p m t -> p (m t)")
+            nc.sync.dma_start(out=dst.bitcast(I32), in_=y_codes[g][:, tokens].bitcast(I32))
 
         def store_scales(a):
             for q in range(QUADRANTS):
@@ -240,34 +253,32 @@ def tile_squared_relu_up_projection_b1_kernel(tc, X_bytes, X_scale, W, b, out_0,
                 queue = nc.scalar if q % 2 and (a + 1) * PACKED == GROUPS else nc.sync
                 queue.dma_start(out=dst.bitcast(I32), in_=y_scales[a][32 * q:32 * q + 4 * PACKED, :].bitcast(I32))
 
-        def quantize_y(g, first, end):
+        def quantize_y(g, first, end, from_gpsimd=False):
             if g not in y_codes:
                 y_codes[g] = work.tile([P, T], U32, name="y_codes", bufs=RESULT_SLOTS // 2, align_bytes=64)
             plane = y_scales[g // PACKED][4 * (g % PACKED):, :]
             nc.vector.quantize_mx(out=y_codes[g][:, first:end].bitcast(FP8X4), scales=plane[:, first:end],
-                                  in_=y_bf16[g][:, first * PACK:end * PACK])
+                                  in_=y_gpsimd if from_gpsimd else y_bf16[g][:, first * PACK:end * PACK])
 
         def quantize_planes(step):
             g, h = divmod(step, 2)
             if g == GROUPS - 1:
+                tokens = slice(h * HALF, (h + 1) * HALF)
                 for run in RUNS:
-                    quantize_y(g, h * HALF + run.start, h * HALF + run.stop)
-            elif h == 0:
-                quantize_y(g, 0, RUNS[0].stop)
+                    quantize_y(g, tokens.start + run.start, tokens.start + run.stop,
+                               step in GPSIMD_STEPS and run == RUNS[1])
+            elif step in GPSIMD_STEPS:
+                tokens = slice(RUNS[0].stop, T)
+                quantize_y(g, tokens.start, T - 2 * P)
+                quantize_y(g, T - P, T, True)
+                quantize_y(g, T - 2 * P, T - P)
             else:
-                quantize_y(g, RUNS[0].stop, T)
-            store_planes(step)
-
-        def store_planes(step):
-            g, h = divmod(step, 2)
-            if g >= GROUPS - 2 or h == 1:
-                tokens = slice(0, T)
-                if g == GROUPS - 1:
-                    tokens = slice(h * HALF, (h + 1) * HALF)
-                elif g == GROUPS - 2:
-                    tokens = slice(RUNS[0].stop, T) if h else RUNS[0]
-                dst = out_1[g, :, tokens, :].rearrange("p m t -> p (m t)")
-                nc.sync.dma_start(out=dst.bitcast(I32), in_=y_codes[g][:, tokens].bitcast(I32))
+                tokens = slice(RUNS[0].stop, T) if h else RUNS[0]
+                quantize_y(g, tokens.start, tokens.stop)
+            if g >= GROUPS - 2:
+                store_codes(g, tokens)
+            elif h == 1:
+                store_codes(g, slice(0, T))
             if h == 1 and g % PACKED == PACKED - 1:
                 store_scales(g // PACKED)
 
@@ -285,48 +296,46 @@ def tile_squared_relu_up_projection_b1_kernel(tc, X_bytes, X_scale, W, b, out_0,
         interleave_w(1, 1, "scalar")
         widen_x(4, on_vector=True)
         widen_x(5, on_vector=False)
-        warm_up_tensor_engine(w_first[0][:, UNIT_PART:], GROUP, 3)
+        warm_up_tensor_engine(WARM_UPS[0])
         turn_x(3)
         turn_x(4)
-        warm_up_tensor_engine(w_first[0][:, UNIT_PART:], GROUP, 2)
+        warm_up_tensor_engine(WARM_UPS[1])
         quantize_w(0, 0)
         quantize_x(0)
         quantize_w(0, 1)
         quantize_w(1)
         turn_x(5)
-        multiply(0, 0)
-        multiply(0, 1)
-        multiply(0, 2)
-        multiply(0, 3)
-        add_bias_and_clamp(0, range(PACK), on_vector=False)
-        interleave_w(2, 0, "vector")
-        interleave_w(2, 1, "vector")
+        for t in range(PACK):
+            multiply(0, t)
+        add_bias_and_clamp(0, on_vector=False)
+        for c in range(PASSES):
+            interleave_w(W_AHEAD, c, "vector")
         quantize_x(1)
-        quantize_w(2)
-        interleave_w(3, 1, "vector")
+        quantize_w(W_AHEAD)
+        interleave_w(W_AHEAD + 1, 1, "vector")
 
         for step in range(STEPS):
             n = step + W_AHEAD
             last = step == STEPS - 1
             late = step >= FIRST_LATE_STEP
-            if last:
-                for tokens in RUNS:
-                    add_bias_and_clamp(step, range(PACK), on_vector=True, tokens=tokens)
-            elif step > 0:
-                add_bias_and_clamp(step, range(PACK), on_vector=True)
-            if 0 < step and n < UNITS:
-                interleave_w(n, 0, "gpsimd")
-            if 0 < step <= FIRST_LATE_STEP:
-                quantize_planes(step - 1)
-            if 0 < step and n < UNITS:
-                quantize_w(n)
-            if 0 < step and n + 1 < UNITS:
-                interleave_w(n + 1, 1, "vector")
-            if step > FIRST_LATE_STEP:
-                square_for_planes(step - 1, "vector", HALF - vector_tokens(step - 1), HALF)
-            if FIRST_LATE_STEP + 1 < step < STEPS - 1:
-                quantize_planes(step - 2)
-            tiles_between = TILES if step == UNITS - 1 - W_AHEAD else min(step, TILES - 1)
+            if step > 0:
+                for tokens in RUNS if last else (slice(0, HALF),):
+                    add_bias_and_clamp(step, on_vector=True, tokens=tokens)
+                if n < UNITS:
+                    interleave_w(n, 0, "gpsimd")
+                if step <= FIRST_LATE_STEP:
+                    quantize_planes(step - 1)
+                if n < UNITS:
+                    quantize_w(n)
+                if n + 1 < UNITS:
+                    interleave_w(n + 1, 1, "vector")
+                if step - 1 in GPSIMD_STEPS:
+                    square_on_gpsimd(step - 1)
+                if step > FIRST_LATE_STEP:
+                    square_for_planes(step - 1, on_vector=True)
+                if step == FIRST_LATE_STEP + 2:
+                    quantize_planes(FIRST_LATE_STEP)
+            tiles_between = TILES if n == UNITS - 1 else min(step, TILES - 1)
             for t in range(PACK // 2):
                 if not last:
                     multiply(step + 1, t)
@@ -337,17 +346,14 @@ def tile_squared_relu_up_projection_b1_kernel(tc, X_bytes, X_scale, W, b, out_0,
                     multiply(step + 1, t)
             for i in range(tiles_between, TILES):
                 turn_clamped(step, i)
-            if not late:
-                square_for_planes(step, "scalar", 0, HALF)
-            tiles_first = TILES if step % 2 else TILES - 1
-            for i in range(TILES):
-                if late and i == tiles_first:
-                    square_for_planes(step, "scalar", 0, HALF - vector_tokens(step))
-                    if step == STEPS - 2:
-                        quantize_planes(step - 1)
-                square_and_store(step, i, nc.sync)
-            if late and tiles_first == TILES:
-                square_for_planes(step, "scalar", 0, HALF - vector_tokens(step))
-        square_for_planes(STEPS - 1, "vector", HALF - vector_tokens(STEPS - 1), HALF)
+            tiles_first = (TILES if step % 2 else TILES - 1) if late else 0
+            for i in range(tiles_first):
+                square_and_store(step, i)
+            square_for_planes(step, on_vector=False)
+            if step == STEPS - 2:
+                quantize_planes(step - 1)
+            for i in range(tiles_first, TILES):
+                square_and_store(step, i)
+        square_for_planes(STEPS - 1, on_vector=True)
         quantize_planes(STEPS - 2)
         quantize_planes(STEPS - 1)

@@ -35,7 +35,7 @@ HEAD_SHARE = 40
 FIRST_LATE_STEP = UNITS - W_AHEAD - 2
 VECTOR_TOKENS = (128, 64, 128, 256)
 GPSIMD_STEPS = (STEPS - 3, STEPS - 2)
-WARM_UPS = (3, 2)
+WARM_UPS = (2, 2)
 PACKED = 4
 W_CODE_SLOTS = 6
 RESULT_SLOTS = 6
@@ -58,7 +58,9 @@ def tile_squared_relu_up_projection_b1_kernel(tc, X_bytes, X_scale, W, b, out_0,
 
         x_factor = [keep.tile([P, TILES, K // X_BLOCK], F32, name="x_factor%d" % h) for h in range(2)]
         bias = keep.tile([P, GROUPS, PACK], BF16, name="bias")
-        x_raw = [keep.tile([P, K], U8, name="x_raw%d" % i) for i in range(2 * TILES)]
+        bias_rows = keep.tile([P, GROUP], BF16, name="bias_rows")
+        nc.gpsimd.memset(bias_rows[:], 0.0)
+        x_raw = {}
         w_raw = {}
         x_grouped = [keep.tile([P, PASSES, HALF, PACK], BF16, name="x_grouped%d" % h, align_bytes=64) for h in range(2)]
         x_codes = [keep.tile([P, PASSES, HALF], U32, name="x_codes%d" % h, align_bytes=64) for h in range(2)]
@@ -72,8 +74,11 @@ def tile_squared_relu_up_projection_b1_kernel(tc, X_bytes, X_scale, W, b, out_0,
             rows = X_scale[h * HALF:(h + 1) * HALF, :]
             queue.dma_start(out=x_factor[h][:], in_=rows.rearrange("(i p) j -> p i j", p=P))
 
-        def load_x(i):
-            nc.sync.dma_start(out=x_raw[i][:], in_=X_bytes[i * P:(i + 1) * P, :])
+        def load_x(first, end):
+            tile = keep.tile([P, end - first, K], U8, name="x_raw%d" % first)
+            nc.sync.dma_start(out=tile[:], in_=X_bytes[first * P:end * P, :].rearrange("(i p) k -> p i k", p=P))
+            for i in range(first, end):
+                x_raw[i] = tile[:, i - first, :]
 
         def load_w(first_group, end_group):
             for c in range(PASSES):
@@ -87,17 +92,15 @@ def tile_squared_relu_up_projection_b1_kernel(tc, X_bytes, X_scale, W, b, out_0,
         load_x_factor(0, nc.scalar)
         table_warm_up = keep.tile([P, 1], F32, name="table_warm_up")
         nc.scalar.activation(out=table_warm_up[:], in_=ident[:, 0:1], func=ACT.Square)
-        for i in range(TILES):
-            load_x(i)
+        load_x(0, 1)
+        load_x(1, 3)
         load_x_factor(1, nc.sync)
-        load_x(TILES)
+        load_x(3, 4)
+        load_x(4, 6)
         load_w(0, 1)
-        for i in range(TILES + 1, 2 * TILES):
-            load_x(i)
+        nc.sync.dma_start(out=bias_rows[:GROUPS, :], in_=b.rearrange("o (g f) -> (o g) f", g=GROUPS))
         for first_group, end_group in W_LOADS:
             load_w(first_group, end_group)
-            if first_group == 1:
-                nc.sync.dma_start(out=bias[:], in_=b.rearrange("o (g p t) -> p (o g) t", p=P, t=PACK))
 
         x_words, w_codes, w_scales = {}, {}, {}
         sum_banks, clamped, turned, y_bf16, y_codes, y_rows = {}, {}, {}, {}, {}, {}
@@ -130,6 +133,17 @@ def tile_squared_relu_up_projection_b1_kernel(tc, X_bytes, X_scale, W, b, out_0,
             pairs = x_grouped[h][:].rearrange("p c m j -> p c (m j)").bitcast(F32).rearrange("p c (m u) -> p c m u", u=2)
             nc.scalar.copy(out=pairs[:, :, first:first + P, :],
                            in_=bank[:].rearrange("p (c u m) -> p c m u", c=PASSES, u=2))
+
+        def turn_bias():
+            bank = psum.tile([P, GROUP], F32, name="turn")
+            words = bias_rows[:].bitcast(F32)
+            for u in range(2):
+                nc.tensor.transpose(bank[:, u * P:(u + 1) * P], words[:, u:2 * P:2], ident[:])
+            return bank
+
+        def copy_bias(bank):
+            nc.scalar.copy(out=bias[:].bitcast(F32),
+                           in_=bank[:, :2 * P].rearrange("p (u g) -> p g u", u=2)[:, :GROUPS, :])
 
         def quantize_x(h):
             codes = x_codes[h][:].rearrange("p c m -> p (c m)")
@@ -284,32 +298,27 @@ def tile_squared_relu_up_projection_b1_kernel(tc, X_bytes, X_scale, W, b, out_0,
 
         widen_x(0, on_vector=True)
         widen_x(1, on_vector=False)
-        widen_x(2, on_vector=True)
-        widen_x(3, on_vector=True)
+        for i in range(2, 2 * TILES):
+            widen_x(i, on_vector=True)
+        for i in (0, 2, 1, 3, 4, 5):
+            turn_x(i)
         interleave_w(0, 0, "vector")
-        interleave_w(1, 0, "vector", slice(HEAD_SHARE, P))
-        turn_x(0)
-        turn_x(2)
-        interleave_w(1, 0, "scalar", slice(0, HEAD_SHARE))
-        turn_x(1)
+        interleave_w(1, 0, "vector", slice(0, P))
         interleave_w(0, 1, "vector")
         interleave_w(1, 1, "scalar")
-        widen_x(4, on_vector=True)
-        widen_x(5, on_vector=False)
         warm_up_tensor_engine(WARM_UPS[0])
-        turn_x(3)
-        turn_x(4)
+        bias_bank = turn_bias()
         warm_up_tensor_engine(WARM_UPS[1])
         quantize_w(0, 0)
         quantize_x(0)
         quantize_w(0, 1)
         quantize_w(1)
-        turn_x(5)
+        interleave_w(W_AHEAD, 0, "scalar", slice(0, 128))
+        copy_bias(bias_bank)
         for t in range(PACK):
             multiply(0, t)
         add_bias_and_clamp(0, on_vector=False)
-        for c in range(PASSES):
-            interleave_w(W_AHEAD, c, "vector")
+        interleave_w(W_AHEAD, 1, "vector")
         quantize_x(1)
         quantize_w(W_AHEAD)
         interleave_w(W_AHEAD + 1, 1, "vector")

@@ -67,7 +67,7 @@ def tile_squared_relu_up_projection_b1_kernel(tc, X_bytes, X_scale, W, b, out_0,
         x_scales = [keep.tile([P, PASSES, HALF], U8, name="x_scales%d" % h, align_bytes=64) for h in range(2)]
         w_first = [keep.tile([P, PASSES * UNIT_PART], BF16, name="w_first%d" % n, align_bytes=64) for n in range(W_AHEAD)]
         w_shared = keep.tile([P, 3 * UNIT_PART], BF16, name="w_shared", align_bytes=64)
-        y_gpsimd = w_shared[:, UNIT_PART:UNIT_PART + P * PACK]
+        y_gpsimd = w_shared[:, UNIT_PART:2 * UNIT_PART]
         y_scales = [keep.tile([P, T], U8, name="y_scales%d" % a, align_bytes=64) for a in range(GROUPS // PACKED)]
 
         def load_x_factor(h, queue):
@@ -204,11 +204,11 @@ def tile_squared_relu_up_projection_b1_kernel(tc, X_bytes, X_scale, W, b, out_0,
                                         rhs=x_codes[h][:, c, run].bitcast(FP8X4), rhs_scale=x_scales[h][:, c, run],
                                         start=(c == 0), stop=(c == PASSES - 1))
 
-        def add_bias_and_clamp(step, on_vector, tokens=slice(0, HALF)):
+        def add_bias_and_clamp(step, on_vector, tokens=slice(0, HALF), slices=range(PACK)):
             g = step // 2
             if step not in clamped:
                 clamped[step] = work.tile([P, PACK, HALF], F32, name="clamped")
-            for t in range(PACK):
+            for t in slices:
                 src, dst = sum_banks[step, t][:, tokens], clamped[step][:, t, tokens]
                 if on_vector:
                     nc.vector.tensor_scalar(out=dst, in0=src, scalar1=bias[:, g, t:t + 1], scalar2=0.0,
@@ -222,15 +222,10 @@ def tile_squared_relu_up_projection_b1_kernel(tc, X_bytes, X_scale, W, b, out_0,
             for t in range(PACK):
                 nc.tensor.transpose(bank[:, t * P:(t + 1) * P], clamped[step][:, t, i * P:(i + 1) * P], ident[:])
 
-        def plane_shares(step):
-            end = RUNS[0].stop if step in GPSIMD_STEPS else HALF
-            return end - (VECTOR_TOKENS[step - FIRST_LATE_STEP] if step >= FIRST_LATE_STEP else 0), end
-
-        def square_for_planes(step, on_vector):
+        def square_for_planes(step, on_vector, first=0, end=HALF):
             g, h = divmod(step, 2)
             if g not in y_bf16:
                 y_bf16[g] = work.tile([P, PACK * T], BF16, name="y_bf16", bufs=PLANE_SLOTS, align_bytes=64)
-            first, end = plane_shares(step) if on_vector else (0, plane_shares(step)[0])
             dst = y_bf16[g][:, (h * HALF + first) * PACK:(h * HALF + end) * PACK]
             dst = dst.rearrange("p (a i t) -> p a t i", i=4, t=PACK)
             src = clamped[step][:, :, first:end].rearrange("p t (a i) -> p a t i", i=4)
@@ -239,23 +234,22 @@ def tile_squared_relu_up_projection_b1_kernel(tc, X_bytes, X_scale, W, b, out_0,
             else:
                 nc.scalar.activation(out=dst, in_=src, func=ACT.Square)
 
-        def square_on_gpsimd(step):
-            dst = y_gpsimd.rearrange("p (a i t) -> p a t i", i=4, t=PACK)
-            src = clamped[step][:, :, RUNS[1]].rearrange("p t (a i) -> p a t i", i=4)
+        def square_on_gpsimd(step, first, end):
+            dst = y_gpsimd[:, :(end - first) * PACK].rearrange("p (a i t) -> p a t i", i=4, t=PACK)
+            src = clamped[step][:, :, first:end].rearrange("p t (a i) -> p a t i", i=4)
             nc.gpsimd.tensor_tensor(out=dst, in0=src, in1=src, op=ALU.mult)
 
-        def square_and_store(step, i):
-            g, h = divmod(step, 2)
+        def square_tile(step, i):
             if i == 0:
                 y_rows[step] = work.tile([P, TILES, GROUP], F32, name="y", bufs=RESULT_SLOTS)
             y = y_rows[step]
             nc.scalar.activation(out=y[:, i, :].rearrange("p (m t) -> p m t", t=PACK),
                                  in_=turned[step, i][:].rearrange("p (t m) -> p m t", t=PACK), func=ACT.Square)
+
+        def store_y(step, first=0, end=TILES):
+            g, h = divmod(step, 2)
             dst = out_0[h * HALF:(h + 1) * HALF, g * GROUP:(g + 1) * GROUP].rearrange("(i p) f -> p i f", p=P)
-            if step > LAST_WHOLE_STORE:
-                nc.sync.dma_start(out=dst[:, i, :], in_=y[:, i, :])
-            elif i == TILES - 1:
-                nc.sync.dma_start(out=dst, in_=y[:])
+            nc.sync.dma_start(out=dst[:, first:end, :], in_=y_rows[step][:, first:end, :])
 
         def store_codes(g, tokens):
             dst = out_1[g, :, tokens, :].rearrange("p m t -> p (m t)")
@@ -272,29 +266,16 @@ def tile_squared_relu_up_projection_b1_kernel(tc, X_bytes, X_scale, W, b, out_0,
                 y_codes[g] = work.tile([P, T], U32, name="y_codes", bufs=RESULT_SLOTS // 2, align_bytes=64)
             plane = y_scales[g // PACKED][4 * (g % PACKED):, :]
             nc.vector.quantize_mx(out=y_codes[g][:, first:end].bitcast(FP8X4), scales=plane[:, first:end],
-                                  in_=y_gpsimd if from_gpsimd else y_bf16[g][:, first * PACK:end * PACK])
+                                  in_=y_gpsimd[:, :(end - first) * PACK] if from_gpsimd else y_bf16[g][:, first * PACK:end * PACK])
 
         def quantize_planes(step):
             g, h = divmod(step, 2)
-            if g == GROUPS - 1:
-                tokens = slice(h * HALF, (h + 1) * HALF)
-                for run in RUNS:
-                    quantize_y(g, tokens.start + run.start, tokens.start + run.stop,
-                               step in GPSIMD_STEPS and run == RUNS[1])
-            elif step in GPSIMD_STEPS:
-                tokens = slice(RUNS[0].stop, T)
-                quantize_y(g, tokens.start, T - 2 * P)
-                quantize_y(g, T - P, T, True)
-                quantize_y(g, T - 2 * P, T - P)
-            else:
-                tokens = slice(RUNS[0].stop, T) if h else RUNS[0]
-                quantize_y(g, tokens.start, tokens.stop)
-            if g >= GROUPS - 2:
-                store_codes(g, tokens)
-            elif h == 1:
+            tokens = slice(RUNS[0].stop, T) if h else RUNS[0]
+            quantize_y(g, tokens.start, tokens.stop)
+            if h == 1:
                 store_codes(g, slice(0, T))
-            if h == 1 and g % PACKED == PACKED - 1:
-                store_scales(g // PACKED)
+                if g % PACKED == PACKED - 1:
+                    store_scales(g // PACKED)
 
         widen_x(0, on_vector=True)
         widen_x(1, on_vector=False)
@@ -323,46 +304,109 @@ def tile_squared_relu_up_projection_b1_kernel(tc, X_bytes, X_scale, W, b, out_0,
         quantize_w(W_AHEAD)
         interleave_w(W_AHEAD + 1, 1, "vector")
 
-        for step in range(STEPS):
+        for step in range(12):
             n = step + W_AHEAD
-            last = step == STEPS - 1
-            late = step >= FIRST_LATE_STEP
             if step > 0:
-                for tokens in RUNS if last else (slice(0, HALF),):
-                    add_bias_and_clamp(step, on_vector=True, tokens=tokens)
-                if n < UNITS:
-                    interleave_w(n, 0, "gpsimd")
-                if step <= FIRST_LATE_STEP:
-                    quantize_planes(step - 1)
-                if n < UNITS:
-                    quantize_w(n)
-                if n + 1 < UNITS:
-                    interleave_w(n + 1, 1, "vector")
-                if step - 1 in GPSIMD_STEPS:
-                    square_on_gpsimd(step - 1)
-                if step > FIRST_LATE_STEP:
-                    square_for_planes(step - 1, on_vector=True)
-                if step == FIRST_LATE_STEP + 2:
-                    quantize_planes(FIRST_LATE_STEP)
-            tiles_between = TILES if n == UNITS - 1 else min(step, TILES - 1)
+                add_bias_and_clamp(step, on_vector=True)
+                interleave_w(n, 0, "gpsimd")
+                quantize_planes(step - 1)
+                quantize_w(n)
+                interleave_w(n + 1, 1, "vector")
+            tiles_between = min(step, TILES - 1)
             for t in range(PACK // 2):
-                if not last:
-                    multiply(step + 1, t)
+                multiply(step + 1, t)
             for i in range(tiles_between):
                 turn_clamped(step, i)
             for t in range(PACK // 2, PACK):
-                if not last:
-                    multiply(step + 1, t)
+                multiply(step + 1, t)
             for i in range(tiles_between, TILES):
                 turn_clamped(step, i)
-            tiles_first = (TILES if step % 2 else TILES - 1) if late else 0
-            for i in range(tiles_first):
-                square_and_store(step, i)
             square_for_planes(step, on_vector=False)
-            if step == STEPS - 2:
-                quantize_planes(step - 1)
-            for i in range(tiles_first, TILES):
-                square_and_store(step, i)
-        square_for_planes(STEPS - 1, on_vector=True)
-        quantize_planes(STEPS - 2)
-        quantize_planes(STEPS - 1)
+            for i in range(TILES):
+                square_tile(step, i)
+                if step > LAST_WHOLE_STORE:
+                    store_y(step, i, i + 1)
+            if step <= LAST_WHOLE_STORE:
+                store_y(step)
+
+        add_bias_and_clamp(12, True)
+        interleave_w(14, 0, "gpsimd")
+        quantize_planes(11)
+        quantize_w(14)
+        interleave_w(15, 1, "vector")
+        multiply(13, 0)
+        multiply(13, 1)
+        turn_clamped(12, 0)
+        turn_clamped(12, 1)
+        multiply(13, 2)
+        multiply(13, 3)
+        turn_clamped(12, 2)
+        square_tile(12, 0)
+        store_y(12, 0, 1)
+        square_tile(12, 1)
+        store_y(12, 1, 2)
+        square_for_planes(12, False, 0, 384)
+        square_tile(12, 2)
+        store_y(12, 2, 3)
+        add_bias_and_clamp(13, True)
+        interleave_w(15, 0, "gpsimd")
+        quantize_w(15)
+        quantize_y(6, 0, 256)
+        multiply(14, 0)
+        multiply(14, 1)
+        turn_clamped(13, 0)
+        turn_clamped(13, 1)
+        turn_clamped(13, 2)
+        multiply(14, 2)
+        multiply(14, 3)
+        square_tile(13, 0)
+        store_y(13, 0, 1)
+        store_codes(6, slice(0, 256))
+        square_tile(13, 1)
+        store_y(13, 1, 2)
+        square_tile(13, 2)
+        store_y(13, 2, 3)
+        add_bias_and_clamp(14, True)
+        square_on_gpsimd(13, 256, 384)
+        multiply(15, 0)
+        multiply(15, 1)
+        turn_clamped(14, 0)
+        turn_clamped(14, 1)
+        multiply(15, 2)
+        multiply(15, 3)
+        turn_clamped(14, 2)
+        square_for_planes(13, False, 128, 256)
+        square_for_planes(14, False, 0, 128)
+        square_for_planes(13, True, 0, 128)
+        quantize_y(6, 512, 640)
+        quantize_y(6, 640, 768, True)
+        quantize_y(6, 256, 512)
+        store_codes(6, slice(256, 768))
+        square_tile(14, 0)
+        store_y(14, 0, 1)
+        square_tile(14, 1)
+        store_y(14, 1, 2)
+        square_for_planes(14, False, 128, 256)
+        square_tile(14, 2)
+        store_y(14, 2, 3)
+        add_bias_and_clamp(15, True, slice(0, 256))
+        square_on_gpsimd(14, 256, 384)
+        add_bias_and_clamp(15, True, slice(256, 384))
+        turn_clamped(15, 0)
+        turn_clamped(15, 1)
+        turn_clamped(15, 2)
+        quantize_y(7, 0, 256)
+        quantize_y(7, 256, 384, True)
+        square_for_planes(15, True, 0, 128)
+        square_tile(15, 0)
+        store_y(15, 0, 1)
+        square_tile(15, 1)
+        store_y(15, 1, 2)
+        square_tile(15, 2)
+        store_y(15, 2, 3)
+        square_for_planes(15, True, 128, 320)
+        quantize_y(7, 384, 512)
+        square_for_planes(15, False, 320, 384)
+        quantize_y(7, 512, 768)
+        store_codes(7, slice(0, 768))
+        store_scales(1)

@@ -312,7 +312,7 @@ def tile_squared_relu_up_projection_b1_kernel(tc, X_bytes, X_scale, W, b, out_0,
                 quantize_planes(step - 1)
                 quantize_w(n)
                 interleave_w(n + 1, 1, "vector")
-            tiles_between = min(step, TILES - 1)
+            tiles_between = step if step < 2 else TILES
             for t in range(PACK // 2):
                 multiply(step + 1, t)
             for i in range(tiles_between):
@@ -338,9 +338,9 @@ def tile_squared_relu_up_projection_b1_kernel(tc, X_bytes, X_scale, W, b, out_0,
         multiply(13, 1)
         turn_clamped(12, 0)
         turn_clamped(12, 1)
+        turn_clamped(12, 2)
         multiply(13, 2)
         multiply(13, 3)
-        turn_clamped(12, 2)
         square_tile(12, 0)
         store_y(12, 0, 1)
         square_tile(12, 1)

from contextlib import ExitStack

import concourse.mybir as mybir
from concourse.masks import make_identity

T, K, F = 768, 1024, 4096
FLOPS = 2 * T * K * F

F32 = mybir.dt.float32
BF16 = mybir.dt.bfloat16
I32 = mybir.dt.int32
U32 = mybir.dt.uint32
U8 = mybir.dt.uint8
FP8 = mybir.dt.float8_e4m3fn
FP8X4 = mybir.dt.float8_e4m3fn_x4
ACT = mybir.ActivationFunctionType
ALU = mybir.AluOpType

P = 128
PACK = 4
GROUP = P * PACK
PASSES = K // GROUP
GROUPS = F // GROUP
UNITS = 2 * GROUPS
UNIT_PART = 2 * P * PACK
HALF = T // 2
TILES = HALF // P
STEPS = 2 * GROUPS
RUNS = (slice(0, 256), slice(256, HALF))
X_BLOCK = 128
QUADRANTS = 4

W_AHEAD = 2
HEAD_SHARE = 40
FIRST_LATE_STEP = UNITS - W_AHEAD - 2
VECTOR_TOKENS = (128, 64, 128, 256)
GPSIMD_STEPS = (STEPS - 3, STEPS - 2)
WARM_UPS = (2, 2)
PACKED = 4
W_CODE_SLOTS = 6
RESULT_SLOTS = 6
CLAMPED_SLOTS = 3
PLANE_SLOTS = 2
W_LOADS = ((1, 2), (2, 4), (4, 8))
LAST_WHOLE_STORE = STEPS // 2 - 1


def tile_squared_relu_up_projection_b1_kernel(tc, X_bytes, X_scale, W, b, out_0, out_1, out_2):
    nc = tc.nc
    with ExitStack() as ctx:
        keep = ctx.enter_context(tc.tile_pool(name="keep", bufs=1))
        work = ctx.enter_context(tc.tile_pool(name="work", bufs=CLAMPED_SLOTS))
        psum = ctx.enter_context(tc.psum_pool(name="psum", bufs=4))
        ctx.enter_context(tc.manual_schedule())

        ident = keep.tile([P, P], F32, name="ident")
        make_identity(nc, ident[:])

        x_factor = [keep.tile([P, TILES, K // X_BLOCK], F32, name="x_factor%d" % h) for h in range(2)]
        bias = keep.tile([P, GROUPS, PACK], BF16, name="bias")
        bias_rows = keep.tile([P, GROUP], BF16, name="bias_rows")
        nc.gpsimd.memset(bias_rows[:], 0.0)
        x_raw = {}
        w_raw = {}
        x_grouped = [keep.tile([P, PASSES, HALF, PACK], BF16, name="x_grouped%d" % h, align_bytes=64) for h in range(2)]
        x_codes = [keep.tile([P, PASSES, HALF], U32, name="x_codes%d" % h, align_bytes=64) for h in range(2)]
        x_scales = [keep.tile([P, PASSES, HALF], U8, name="x_scales%d" % h, align_bytes=64) for h in range(2)]
        w_first = [keep.tile([P, PASSES * UNIT_PART], BF16, name="w_first%d" % n, align_bytes=64) for n in range(W_AHEAD)]
        w_shared = keep.tile([P, 3 * UNIT_PART], BF16, name="w_shared", align_bytes=64)
        y_gpsimd = w_shared[:, UNIT_PART:2 * UNIT_PART]
        y_scales = [keep.tile([P, T], U8, name="y_scales%d" % a, align_bytes=64) for a in range(GROUPS // PACKED)]

        def load_x_factor(h, queue):
            rows = X_scale[h * HALF:(h + 1) * HALF, :]
            queue.dma_start(out=x_factor[h][:], in_=rows.rearrange("(i p) j -> p i j", p=P))

        def load_x(first, end):
            tile = keep.tile([P, end - first, K], U8, name="x_raw%d" % first)
            nc.sync.dma_start(out=tile[:], in_=X_bytes[first * P:end * P, :].rearrange("(i p) k -> p i k", p=P))
            for i in range(first, end):
                x_raw[i] = tile[:, i - first, :]

        def load_w(first_group, end_group):
            for c in range(PASSES):
                width = (end_group - first_group) * GROUP
                tile = keep.tile([P, PACK, width], BF16, name="w_raw%d_%d" % (first_group, c))
                rows = W[c * GROUP:(c + 1) * GROUP, first_group * GROUP:end_group * GROUP]
                nc.sync.dma_start(out=tile[:], in_=rows.rearrange("(p j) n -> p j n", j=PACK))
                for g in range(first_group, end_group):
                    w_raw[g, c] = tile[:, :, (g - first_group) * GROUP:(g - first_group + 1) * GROUP]

        load_x_factor(0, nc.scalar)
        table_warm_up = keep.tile([P, 1], F32, name="table_warm_up")
        nc.scalar.activation(out=table_warm_up[:], in_=ident[:, 0:1], func=ACT.Square)
        load_x(0, 1)
        load_x(1, 3)
        load_x_factor(1, nc.sync)
        load_x(3, 4)
        load_x(4, 6)
        load_w(0, 1)
        nc.sync.dma_start(out=bias_rows[:GROUPS, :], in_=b.rearrange("o (g f) -> (o g) f", g=GROUPS))
        for first_group, end_group in W_LOADS:
            load_w(first_group, end_group)

        x_words, w_codes, w_scales = {}, {}, {}
        sum_banks, clamped, turned, y_bf16, y_codes, y_rows = {}, {}, {}, {}, {}, {}

        def widen_x(i, on_vector):
            for c in range(PASSES):
                wide = work.tile([P, GROUP], BF16, name="x_wide", bufs=PASSES * 2 * TILES)
                for r in range(GROUP // X_BLOCK):
                    block = c * (GROUP // X_BLOCK) + r
                    src = x_raw[i][:, block * X_BLOCK:(block + 1) * X_BLOCK].bitcast(FP8)
                    factor = x_factor[i // TILES][:, i % TILES, block:block + 1]
                    if on_vector:
                        dst = wide[:].rearrange("p (u r a e) -> p r a u e", u=2, r=GROUP // X_BLOCK, e=2)[:, r]
                        nc.vector.tensor_scalar(out=dst, in0=src.rearrange("p (a u e) -> p a u e", u=2, e=2),
                                                scalar1=factor, scalar2=None, op0=ALU.mult)
                    else:
                        nc.scalar.activation(out=wide[:, r * X_BLOCK:(r + 1) * X_BLOCK], in_=src,
                                             func=ACT.Copy, scale=factor)
                words = wide[:].bitcast(F32)
                for u in range(2):
                    x_words[i, c, u] = words[:, u * P:(u + 1) * P] if on_vector else words[:, u:2 * P:2]

        def turn_x(i):
            h, first = i // TILES, i % TILES * P
            bank = psum.tile([P, GROUP], F32, name="turn")
            for c in range(PASSES):
                for u in range(2):
                    col = (2 * c + u) * P
                    nc.tensor.transpose(bank[:, col:col + P], x_words[i, c, u], ident[:])
            pairs = x_grouped[h][:].rearrange("p c m j -> p c (m j)").bitcast(F32).rearrange("p c (m u) -> p c m u", u=2)
            nc.scalar.copy(out=pairs[:, :, first:first + P, :],
                           in_=bank[:].rearrange("p (c u m) -> p c m u", c=PASSES, u=2))

        def turn_bias():
            bank = psum.tile([P, GROUP], F32, name="turn")
            words = bias_rows[:].bitcast(F32)
            for u in range(2):
                nc.tensor.transpose(bank[:, u * P:(u + 1) * P], words[:, u:2 * P:2], ident[:])
            return bank

        def copy_bias(bank):
            nc.scalar.copy(out=bias[:].bitcast(F32),
                           in_=bank[:, :2 * P].rearrange("p (u g) -> p g u", u=2)[:, :GROUPS, :])

        def quantize_x(h):
            codes = x_codes[h][:].rearrange("p c m -> p (c m)")
            scales = x_scales[h][:].rearrange("p c m -> p (c m)")
            values = x_grouped[h][:].rearrange("p c m j -> p (c m) j")
            for run in (slice(0, GROUP), slice(GROUP, PASSES * HALF)):
                nc.vector.quantize_mx(out=codes[:, run].bitcast(FP8X4), scales=scales[:, run],
                                      in_=values[:, run, :].rearrange("p m j -> p (m j)"))

        def place_of_pass(n, c):
            return c if n % 2 else 1 - c

        def w_grouped(n):
            if n < W_AHEAD:
                return w_first[n][:]
            return w_shared[:, n % 2 * UNIT_PART:(n % 2 + PASSES) * UNIT_PART]

        def interleave_w(n, c, engine, m_range=slice(0, P)):
            g, v = divmod(n, 2)
            first = place_of_pass(n, c) * UNIT_PART
            dst = w_grouped(n)[:, first:first + UNIT_PART].rearrange("p (e m j) -> p m j e", e=2, j=PACK)
            src = w_raw[g, c].rearrange("p j (m v e) -> p v m j e", v=2, e=2)[:, v]
            dst, src = dst[:, m_range], src[:, m_range]
            if engine == "gpsimd":
                nc.gpsimd.tensor_scalar(out=dst.rearrange("p m j e -> p m e j"), in0=src.rearrange("p m j e -> p m e j"),
                                        scalar1=1.0, scalar2=0.0, op0=ALU.mult, op1=ALU.add)
            elif engine == "scalar":
                nc.scalar.copy(out=dst, in_=src)
            else:
                nc.vector.tensor_copy(out=dst, in_=src)

        def quantize_w(n, c=None):
            if n not in w_codes:
                w_codes[n] = work.tile([P, GROUP], U32, name="w_codes", bufs=W_CODE_SLOTS, align_bytes=64)
                w_scales[n] = work.tile([P, GROUP], U8, name="w_scales", bufs=W_CODE_SLOTS, align_bytes=64)
            first, end = (0, PASSES) if c is None else (place_of_pass(n, c), place_of_pass(n, c) + 1)
            words = slice(first * 2 * P, end * 2 * P)
            nc.vector.quantize_mx(out=w_codes[n][:, words].bitcast(FP8X4), scales=w_scales[n][:, words],
                                  in_=w_grouped(n)[:, first * UNIT_PART:end * UNIT_PART])

        def warm_up_tensor_engine(count):
            operand = w_first[0][:, UNIT_PART:]
            bank = psum.tile([P, GROUP], F32, name="sums")
            for r in range(count):
                nc.tensor.matmul(bank[:], lhsT=operand[:, :P], rhs=operand[:, :GROUP], start=True, stop=True)

        def multiply(step, t):
            g, h = divmod(step, 2)
            bank = psum.tile([P, GROUP], F32, name="sums")
            sum_banks[step, t] = bank
            n = 2 * g + t // 2
            for run in RUNS:
                for c in range(PASSES):
                    first = (2 * place_of_pass(n, c) + t % 2) * P
                    cols = slice(first, first + P)
                    nc.tensor.matmul_mx(out=bank[:, run],
                                        lhsT=w_codes[n][:, cols].bitcast(FP8X4), lhsT_scale=w_scales[n][:, cols],
                                        rhs=x_codes[h][:, c, run].bitcast(FP8X4), rhs_scale=x_scales[h][:, c, run],
                                        start=(c == 0), stop=(c == PASSES - 1))

        def add_bias_and_clamp(step, on_vector, tokens=slice(0, HALF), slices=range(PACK)):
            g = step // 2
            if step not in clamped:
                clamped[step] = work.tile([P, PACK, HALF], F32, name="clamped")
            for t in slices:
                src, dst = sum_banks[step, t][:, tokens], clamped[step][:, t, tokens]
                if on_vector:
                    nc.vector.tensor_scalar(out=dst, in0=src, scalar1=bias[:, g, t:t + 1], scalar2=0.0,
                                            op0=ALU.add, op1=ALU.max)
                else:
                    nc.scalar.activation(out=dst, in_=src, func=ACT.Relu, bias=bias[:, g, t:t + 1])

        def turn_clamped(step, i):
            bank = psum.tile([P, GROUP], F32, name="turn")
            turned[step, i] = bank
            for t in range(PACK):
                nc.tensor.transpose(bank[:, t * P:(t + 1) * P], clamped[step][:, t, i * P:(i + 1) * P], ident[:])

        def square_for_planes(step, on_vector, first=0, end=HALF):
            g, h = divmod(step, 2)
            if g not in y_bf16:
                y_bf16[g] = work.tile([P, PACK * T], BF16, name="y_bf16", bufs=PLANE_SLOTS, align_bytes=64)
            dst = y_bf16[g][:, (h * HALF + first) * PACK:(h * HALF + end) * PACK]
            dst = dst.rearrange("p (a i t) -> p a t i", i=4, t=PACK)
            src = clamped[step][:, :, first:end].rearrange("p t (a i) -> p a t i", i=4)
            if on_vector:
                nc.vector.tensor_tensor(out=dst, in0=src, in1=src, op=ALU.mult)
            else:
                nc.scalar.activation(out=dst, in_=src, func=ACT.Square)

        def square_on_gpsimd(step, first, end):
            dst = y_gpsimd[:, :(end - first) * PACK].rearrange("p (a i t) -> p a t i", i=4, t=PACK)
            src = clamped[step][:, :, first:end].rearrange("p t (a i) -> p a t i", i=4)
            nc.gpsimd.tensor_tensor(out=dst, in0=src, in1=src, op=ALU.mult)

        def square_tile(step, i):
            if i == 0:
                y_rows[step] = work.tile([P, TILES, GROUP], F32, name="y", bufs=RESULT_SLOTS)
            y = y_rows[step]
            nc.scalar.activation(out=y[:, i, :].rearrange("p (m t) -> p m t", t=PACK),
                                 in_=turned[step, i][:].rearrange("p (t m) -> p m t", t=PACK), func=ACT.Square)

        def store_y(step, first=0, end=TILES):
            g, h = divmod(step, 2)
            dst = out_0[h * HALF:(h + 1) * HALF, g * GROUP:(g + 1) * GROUP].rearrange("(i p) f -> p i f", p=P)
            nc.sync.dma_start(out=dst[:, first:end, :], in_=y_rows[step][:, first:end, :])

        def store_codes(g, tokens):
            dst = out_1[g, :, tokens, :].rearrange("p m t -> p (m t)")
            nc.sync.dma_start(out=dst.bitcast(I32), in_=y_codes[g][:, tokens].bitcast(I32))

        def store_scales(a):
            for q in range(QUADRANTS):
                dst = out_2[a * PACKED:(a + 1) * PACKED, 4 * q:4 * q + 4, :]
                queue = nc.scalar if q % 2 and (a + 1) * PACKED == GROUPS else nc.sync
                queue.dma_start(out=dst.bitcast(I32), in_=y_scales[a][32 * q:32 * q + 4 * PACKED, :].bitcast(I32))

        def quantize_y(g, first, end, from_gpsimd=False):
            if g not in y_codes:
                y_codes[g] = work.tile([P, T], U32, name="y_codes", bufs=RESULT_SLOTS // 2, align_bytes=64)
            plane = y_scales[g // PACKED][4 * (g % PACKED):, :]
            nc.vector.quantize_mx(out=y_codes[g][:, first:end].bitcast(FP8X4), scales=plane[:, first:end],
                                  in_=y_gpsimd[:, :(end - first) * PACK] if from_gpsimd else y_bf16[g][:, first * PACK:end * PACK])

        def quantize_planes(step):
            g, h = divmod(step, 2)
            tokens = slice(RUNS[0].stop, T) if h else RUNS[0]
            quantize_y(g, tokens.start, tokens.stop)
            if h == 1:
                store_codes(g, slice(0, T))
                if g % PACKED == PACKED - 1:
                    store_scales(g // PACKED)

        widen_x(0, on_vector=True)
        widen_x(1, on_vector=False)
        for i in range(2, 2 * TILES):
            widen_x(i, on_vector=True)
        for i in (0, 2, 1, 3, 4, 5):
            turn_x(i)
        interleave_w(0, 0, "vector")
        interleave_w(1, 0, "vector", slice(0, P))
        interleave_w(0, 1, "vector")
        interleave_w(1, 1, "scalar")
        warm_up_tensor_engine(WARM_UPS[0])
        bias_bank = turn_bias()
        warm_up_tensor_engine(WARM_UPS[1])
        quantize_w(0, 0)
        quantize_x(0)
        quantize_w(0, 1)
        quantize_w(1)
        interleave_w(W_AHEAD, 0, "scalar", slice(0, 128))
        copy_bias(bias_bank)
        for t in range(PACK):
            multiply(0, t)
        add_bias_and_clamp(0, on_vector=False)
        interleave_w(W_AHEAD, 1, "vector")
        quantize_x(1)
        quantize_w(W_AHEAD)
        interleave_w(W_AHEAD + 1, 1, "vector")

        for step in range(12):
            n = step + W_AHEAD
            if step > 0:
                add_bias_and_clamp(step, on_vector=True)
                interleave_w(n, 0, "gpsimd")
                quantize_planes(step - 1)
                quantize_w(n)
                interleave_w(n + 1, 1, "vector")
            tiles_between = step if step < 2 else TILES
            for t in range(PACK // 2):
                multiply(step + 1, t)
            for i in range(tiles_between):
                turn_clamped(step, i)
            for t in range(PACK // 2, PACK):
                multiply(step + 1, t)
            for i in range(tiles_between, TILES):
                turn_clamped(step, i)
            square_for_planes(step, on_vector=False)
            for i in range(TILES):
                square_tile(step, i)
                if step > LAST_WHOLE_STORE:
                    store_y(step, i, i + 1)
            if step <= LAST_WHOLE_STORE:
                store_y(step)

        add_bias_and_clamp(12, True)
        interleave_w(14, 0, "gpsimd")
        quantize_planes(11)
        quantize_w(14)
        interleave_w(15, 1, "vector")
        multiply(13, 0)
        multiply(13, 1)
        turn_clamped(12, 0)
        turn_clamped(12, 1)
        turn_clamped(12, 2)
        multiply(13, 2)
        multiply(13, 3)
        square_tile(12, 0)
        store_y(12, 0, 1)
        square_tile(12, 1)
        store_y(12, 1, 2)
        square_for_planes(12, False, 0, 384)
        square_tile(12, 2)
        store_y(12, 2, 3)
        add_bias_and_clamp(13, True)
        interleave_w(15, 0, "gpsimd")
        quantize_w(15)
        quantize_y(6, 0, 256)
        multiply(14, 0)
        multiply(14, 1)
        turn_clamped(13, 0)
        turn_clamped(13, 1)
        turn_clamped(13, 2)
        multiply(14, 2)
        multiply(14, 3)
        square_tile(13, 0)
        store_y(13, 0, 1)
        store_codes(6, slice(0, 256))
        square_tile(13, 1)
        store_y(13, 1, 2)
        square_tile(13, 2)
        store_y(13, 2, 3)
        add_bias_and_clamp(14, True)
        square_on_gpsimd(13, 256, 384)
        multiply(15, 0)
        multiply(15, 1)
        turn_clamped(14, 0)
        turn_clamped(14, 1)
        multiply(15, 2)
        multiply(15, 3)
        turn_clamped(14, 2)
        square_for_planes(13, False, 128, 256)
        square_for_planes(14, False, 0, 128)
        square_for_planes(13, True, 0, 128)
        quantize_y(6, 512, 640)
        quantize_y(6, 640, 768, True)
        quantize_y(6, 256, 512)
        store_codes(6, slice(256, 768))
        square_tile(14, 0)
        store_y(14, 0, 1)
        square_tile(14, 1)
        store_y(14, 1, 2)
        square_for_planes(14, False, 128, 256)
        square_tile(14, 2)
        store_y(14, 2, 3)
        add_bias_and_clamp(15, True, slice(0, 256))
        square_on_gpsimd(14, 256, 384)
        add_bias_and_clamp(15, True, slice(256, 384))
        turn_clamped(15, 0)
        turn_clamped(15, 1)
        turn_clamped(15, 2)
        quantize_y(7, 0, 256)
        quantize_y(7, 256, 384, True)
        square_for_planes(15, True, 0, 128)
        square_tile(15, 0)
        store_y(15, 0, 1)
        square_tile(15, 1)
        store_y(15, 1, 2)
        square_tile(15, 2)
        store_y(15, 2, 3)
        square_for_planes(15, True, 128, 320)
        quantize_y(7, 384, 512)
        square_for_planes(15, False, 320, 384)
        quantize_y(7, 512, 768)
        store_codes(7, slice(0, 768))
        store_scales(1)
